import numpy as np, ml_dtypes
CORES = [2,7,18,23,34]
N = 5
BF = ml_dtypes.bfloat16
W, H, P, RO, ST, TH = 3072, 1024, 512, 3, 2, 40
def place(o, i):
    return o[np.arange(8)[None, :, None, None], i]
def ground(rng):
    o = np.argsort(rng.random((8, W)), axis=-1); x = np.zeros((N, 8, 16, W), np.int64); top = np.zeros(8, np.int64)
    for g in range(8):
        m = int(rng.choice(np.array([3, 5, 8]))); c = rng.integers(0, 16, (m, 16)); s = np.linspace(0, m, W, endpoint=False)
        i = np.minimum(s.astype(np.int64), m - 1); f = (s - i)[:, None]
        b = np.rint(c[i] * (1 - f) + c[(i + 1) % m] * f).astype(np.int64).T
        y = b[None] + rng.integers(-1, 2, (N, 16, W))
        y = np.where(rng.random((N, 1, W)) < 0.03, rng.integers(0, 16, (N, 16, W)), y)
        x[:, g] = np.clip(y, 0, 15)[:, :, np.argsort(o[g])]; top[g] = W * 28 // (85 * m)
    return o, top, x
def knot(rng, r, share):
    k = (N, 8, 1, r.shape[3]); p = rng.integers(0, 15, k); q = np.minimum(p + rng.integers(1, 5, k), 15)
    hit = (rng.random(k) < share) & (np.arange(16)[None, None, :, None] == q)
    return np.where(hit, np.take_along_axis(r, p, 2), r)
def walk(rng, o, top, n):
    st = np.floor((rng.random((N, 8, 15, n)) * 1.2 - 0.2) * top[None, :, None, None]).astype(np.int64)
    st = st + np.where(rng.random(st.shape) < 0.01, rng.integers(0, W, st.shape), 0)
    a = rng.integers(0, W, (N, 8, 1, n))
    return knot(rng, place(o, np.concatenate([a, a + np.add.accumulate(st, axis=2)], axis=2) % W), 0.4)
def ladder(rng, lev):
    pm = np.argsort(rng.random((8, 16)), axis=-1)
    return np.clip(lev[:, :, None, :] - 15 * pm[None, :, :, None], 0, 15)
def pack(x, c, r):
    return {"x": np.ascontiguousarray(x.reshape(N, 128, W)).astype(np.float32).astype(BF), "c0": np.ascontiguousarray(c.reshape(N, 128, H)).astype(np.int32),
            "r0": np.ascontiguousarray(r.reshape(N, 128, P)).astype(np.int32)}
def setup_inputs(rng):
    o, top, x = ground(rng)
    return pack(x, walk(rng, o, top, H), walk(rng, o, top, P))
def setup_inputs_ties(rng):
    o = np.argsort(rng.random((8, W)), axis=-1); cls = np.argsort(o, axis=-1) % 7
    cr = np.where(rng.random((N, 8, W)) < 0.04, rng.integers(0, 7, (N, 8, W)), cls[None])
    lev = np.array([0, 1, TH, TH + 1, 2 * TH, 2 * TH + 1, 3 * TH + 2])[cr]
    def some(n):
        i = rng.integers(0, 6, (N, 8, n)); rows = [i]
        for p in range(15):
            jump = rng.random((N, 8, n)) < 0.04
            d = np.where(jump, rng.choice(np.array([-3, 3]), (N, 8, n)), rng.choice(np.array([-2, -2, -1, 0, 1, 2, 2]), (N, 8, n)))
            i = np.clip(i + d, 0, 5 + jump.astype(np.int64)); rows.append(i)
        i = np.stack(rows, axis=2)
        return place(o, i + 7 * rng.integers(0, W // 7, i.shape))
    return pack(ladder(rng, lev), some(H), some(P))
def setup_inputs_clash(rng):
    hi = np.arange(W - 64, W); last6 = (hi[:, None] * hi[None, :]) % 64 == 63; over = last6 & (hi[:, None] * (hi[None, :] + 64) > 2 ** 24)
    hu, hv = np.nonzero(over if np.any(over) else last6)
    nm = rng.random((8, W)) < 0.5; a = rng.integers(1, H - 1, 8); row = np.arange(16)[None, :, None]
    r = np.zeros((N, 8, 16, P), np.int64); c = np.zeros((N, 8, 16, H), np.int64); lev = np.zeros((N, 8, W), np.int64)
    for g in range(8):
        sp = np.array([0, H - 1, int(a[g]), int(a[g]) + H]); nm[g, sp] = True
        apart = rng.permutation(H)[:P] + H * rng.integers(0, 2, P)
        if g == 4: nm[g, apart] = True
        if g == 5: nm[g, W - 64:] = True
        ne, fa = np.flatnonzero(nm[g]), np.flatnonzero(~nm[g])
        if g < 2: u, v = sp[2:], np.array([0, 0])
        elif g < 4: u, v = sp[:2], np.array([int(rng.choice(ne)), 0])
        elif g == 4: u, v = apart, np.zeros(P, np.int64)
        elif g == 5: u, v = hi[hu], hi[hv]
        else: u, v = rng.choice(ne, 8), rng.choice(ne, 8)
        i = rng.integers(0, len(u), (N, P)); k = rng.integers(0, 16, (N, P))
        if g == 4: i = np.argsort(rng.random((N, P)), axis=-1)
        if g == 1 or g == 4: k = rng.integers(0, 14, (N, P))
        if g == 0: k[0, :3] = 15; k[0, 3] = 5; k[1] = 15; k[1, P - 1] = 3
        k[2] = np.minimum(k[2], 14)
        at = np.where(k < 15, k, rng.integers(0, 15, (N, P)))
        y = np.where(row > k[:, None], rng.choice(fa, (N, 16, P)), rng.choice(ne, (N, 16, P)))
        y = np.where(row == at[:, None], u[i][:, None], y)
        y[:, 15] = np.where(k == 14, y[:, 15], v[i]); r[:, g] = y
        flip = rng.random((N, W)) < 0.02; flip[:, sp] = False; flip[:3] = False
        lev[:, g] = np.where(nm[g][None] ^ flip, 0, 150) + rng.integers(0, 6, (N, W))
        c[:, g] = np.where(rng.random((N, 1, H)) < 0.5, rng.choice(ne, (N, 16, H)), rng.integers(0, W, (N, 16, H)))
    return pack(ladder(rng, lev), c, r)
def setup_inputs_loops(rng):
    o, top, x = ground(rng); x[:, ::2] = rng.integers(0, 3, (N, 4, 16, W))
    e = np.argsort(o, axis=-1); b = 1 + 2 * int(rng.integers(0, 4)); z = int(rng.integers(0, N))
    x[:, b] = np.where(e[b] % 3 == 0, rng.integers(0, 3, (N, 16, W)), x[:, b])
    def tie(r):
        kd = rng.integers(0, 8, (N, 8, r.shape[3]))
        for p in range(1, 16):
            r[:, :, p] = np.where(kd == 1, r[:, :, 0], r[:, :, p])
            if p > 1: r[:, :, p] = np.where(kd == 7, r[:, :, p % 2], r[:, :, p])
        for m, dst, src in ((2, 15, 0), (3, 15, 14), (4, 5, 0), (4, 9, 0), (5, 4, 1), (5, 6, 2), (6, 12, 3), (6, 8, 5)):
            r[:, :, dst] = np.where(kd == m, r[:, :, src], r[:, :, dst])
        return r
    w = walk(rng, o, top, P); w[z, b] = o[b][e[b][w[z, b]] // 3 * 3]
    return pack(x, tie(walk(rng, o, top, H)), tie(w))
def setup_inputs_calm(rng):
    o, top, x = ground(rng); q = rng.permutation(N)
    x[q[0]] = rng.integers(0, 3, (8, 16, W)); x[q[1]] = 15 * rng.integers(0, 2, (8, 16, W))
    x[:, int(rng.integers(0, 8))] = rng.integers(0, 3, (N, 16, W))
    e = np.argsort(o, axis=-1); home = e[None] % N == np.arange(N)[:, None, None]
    x = np.where(home[:, :, None], rng.integers(0, 3, x.shape), x)
    i = place(e, walk(rng, o, top, P)) // N * N + np.arange(N)[:, None, None, None]
    return pack(x, walk(rng, o, top, H), place(o, np.where(i < W, i, i - N)))
def setup_inputs_spread(rng):
    o = np.argsort(rng.random((8, W)), axis=-1); e = np.argsort(o, axis=-1) % 5
    x = np.floor(rng.random((N, 8, 16, W)) * np.exp2(4.0 - e)[None, :, None, :]).astype(np.int64)
    def some(n):
        k = rng.integers(0, 4, (N, 8, 1, n)); u = rng.random((N, 8, 16, n)); b = 5 * np.floor(u * (W // 5)).astype(np.int64)
        i = np.where(k == 0, np.floor(W * u).astype(np.int64), np.floor(W * u ** 4).astype(np.int64))
        i = np.where(k == 2, b + rng.integers(3, 5, u.shape), np.where(k == 3, b + rng.integers(2, 5, u.shape), i))
        return place(o, np.minimum(i, W - 1))
    return pack(x, some(H), some(P))
def check_inputs(d):
    bad = []; a = np.asarray(d["x"]).astype(np.float32)
    if not np.all((a >= 0) & (a <= 15) & (a == np.floor(a))): bad.append("whole numbers of x")
    for k in ("c0", "r0"):
        if np.min(d[k]) < 0 or np.max(d[k]) > W - 1: bad.append("range of " + k)
    return bad
def look(xs, R):
    return np.take_along_axis(xs, R.reshape(N, 8, 1, 16 * P), axis=3).reshape(N, 8, 16, 16, P)
def far(v, d):
    return np.add.reduce(np.abs(v[:, :, :, :16 - d] - v[:, :, :, d:]), axis=2)
def first(bad):
    return np.where(np.any(bad, axis=2), np.argmax(bad, axis=2), 15)[:, :, None, :]
def reference(x, c0, r0):
    xs = x.astype(np.float32).astype(np.int32).reshape(N, 8, 16, W); C = c0.astype(np.int64).reshape(N, 8, 16, H).copy()
    R = r0.astype(np.int64).reshape(N, 8, 16, P)
    kap = np.zeros(N, np.int64); row = np.arange(16)[None, None, :, None]
    for rnd in range(RO):
        if rnd > 0: R = np.roll(R, ST, axis=0)
        bad = far(look(xs, R), 1) > TH; fail = np.any(bad, axis=2); k = first(bad)
        rk = np.take_along_axis(R, k, 2)[:, :, 0]
        h = (((rk * R[:, :, 15]) >> 6) + rk + kap[:, None, None]) & (H - 1)
        R = np.where((row > k) & (row < 15), np.take_along_axis(C, h[:, :, None, :], 3), R)
        same = R[:, :, :, None] == R[:, :, None]
        q = 15 - np.argmax(same[:, :, :, ::-1], axis=3)
        p = first((q > row)[:, :, :15])
        R = np.where((row >= p) & (row <= np.take_along_axis(q, p, 2)), np.take_along_axis(R, p, 2), R)
        v = look(xs, R); k2 = first(far(v, 1) > TH)
        S = np.where((row > k2) & (row < 15), np.take_along_axis(R, k2, 2), R)
        for j in range(P - 1, -1, -1):
            a, g = np.nonzero(fail[:, :, j])
            C[a, g, :, h[a, g, j]] = S[:, :, :, j][a, g]
        near = far(v, 2) <= TH; R = R.copy()
        R[:, :, 1:14:2] = np.where(near[:, :, 0:13:2], R[:, :, 0:13:2], R[:, :, 1:14:2])
        kap = np.add.reduce(fail.astype(np.int64), axis=(1, 2))
    return {"yc": C.reshape(N, 128, H).astype(np.float32), "yr": R.reshape(N, 128, P).astype(np.float32)}

@@ -1,0 +1,663 @@
+import math
+from concourse.mybir import AluOpType as A, AxisListType, ActivationFunctionType as F
+
+W, H, P, RO, ST = 3072, 1024, 512, 3, 2
+SH = 1536
+CH = 256
+NC = P // CH
+NL = CH // 16
+RT = 1024 // CH
+KG = 64
+NAD = 4
+
+SCRATCH = {
+    "xs": ("sbuf", [128, W], "bfloat16"), "r0i": ("sbuf", [128, P], "int32"), "c0i": ("sbuf", [128, H], "int32"),
+    "cache": ("sbuf", [128, H + P], "float32"),
+    "va": ("sbuf", [128, 16 * P], "bfloat16"), "vd": ("sbuf", [128, 16 * P], "bfloat16"),
+    "eqw": ("sbuf", [128, 32 * P], "bfloat16"), "eqp": ("sbuf", [128, 2 * 1024 * NC], "bfloat16"),
+    "rf0": ("sbuf", [128, P], "float16"), "rf1": ("sbuf", [128, P], "float16"), "rf2": ("sbuf", [128, P], "float16"),
+    "rn0": ("sbuf", [128, P], "float16"), "rn1": ("sbuf", [128, P], "float16"),
+    "r2": ("sbuf", [128, P], "float16"), "rp": ("sbuf", [128, P], "float16"),
+    "ru": ("sbuf", [128, P], "uint16"), "rpu": ("sbuf", [128, P], "uint16"),
+    "sb": ("sbuf", [128, P], "bfloat16"), "ind": ("sbuf", [128, P], "bfloat16"), "indr": ("sbuf", [128, P], "float16"),
+    "t1": ("sbuf", [128, P], "float32"), "t2": ("sbuf", [128, P], "float32"),
+    "sf": ("sbuf", [128, P], "bfloat16"), "fr": ("sbuf", [128, P], "float16"), "ee": ("sbuf", [128, P], "bfloat16"),
+    "sm": ("sbuf", [128, P], "bfloat16"), "t3": ("sbuf", [128, P], "float32"),
+    "sb2": ("sbuf", [128, P], "bfloat16"), "ind2": ("sbuf", [128, P], "bfloat16"), "indr2": ("sbuf", [128, P], "float16"),
+    "t4": ("sbuf", [128, P], "float32"), "st": ("sbuf", [128, P], "float32"),
+    "sn": ("sbuf", [128, P], "bfloat16"), "t5": ("sbuf", [128, P], "float32"), "yrs": ("sbuf", [128, P], "float32"),
+    "r15": ("sbuf", [128, 32], "float32"), "rk": ("sbuf", [128, 32], "float32"), "rkk": ("sbuf", [128, 32], "float32"),
+    "pri": ("sbuf", [128, 32], "int32"), "fi": ("sbuf", [128, 32], "int32"), "si": ("sbuf", [128, 32], "int32"),
+    "hm": ("sbuf", [128, 32], "int32"), "nfl": ("sbuf", [128, 32], "float32"), "djn": ("sbuf", [128, 32], "float32"),
+    "hf": ("sbuf", [128, 32], "float32"), "hu": ("sbuf", [128, 32], "uint16"), "hh": ("sbuf", [128, 32], "float16"),
+    "hrep": ("sbuf", [128, P], "float16"), "lose": ("sbuf", [128, P], "bfloat16"),
+    "lt": ("sbuf", [128, 32], "float32"), "lo": ("sbuf", [128, 32], "float32"), "wu": ("sbuf", [128, 32], "uint16"),
+    "ksum": ("sbuf", [128, 8], "float32"), "kcol": ("sbuf", [128, 8], "float32"),
+    "ones": ("sbuf", [128, 2048], "bfloat16"), "c1536": ("sbuf", [128, CH], "bfloat16"), "zero": ("sbuf", [128, 8], "bfloat16"),
+    "onesf": ("sbuf", [128, 128], "float32"),
+    "bo": ("sbuf", [128, 128], "bfloat16"), "bo1": ("sbuf", [128, 128], "bfloat16"), "ey": ("sbuf", [128, 128], "bfloat16"),
+    "ney": ("sbuf", [128, 128], "bfloat16"), "ux": ("sbuf", [128, 128], "bfloat16"), "ux8": ("sbuf", [128, 128], "bfloat16"),
+    "wq": ("sbuf", [128, 128], "bfloat16"), "u15": ("sbuf", [128, 128], "bfloat16"), "u15s": ("sbuf", [128, 128], "bfloat16"),
+    "u15n": ("sbuf", [128, 128], "bfloat16"), "tl": ("sbuf", [128, 128], "bfloat16"), "tl2": ("sbuf", [128, 128], "bfloat16"),
+    "au": ("sbuf", [128, 128], "bfloat16"), "au16": ("sbuf", [128, 128], "bfloat16"),
+    "boq": ("sbuf", [128, 128], "bfloat16"), "boqm": ("sbuf", [128, 128], "bfloat16"), "boqp": ("sbuf", [128, 128], "bfloat16"),
+    "hey": ("sbuf", [128, 128], "bfloat16"),
+    "b8a": ("sbuf", [128, 8], "bfloat16"), "b8": ("sbuf", [128, 8], "bfloat16"), "b15": ("sbuf", [128, 8], "bfloat16"),
+    "mst": ("sbuf", [128, 144], "bfloat16"), "mst15": ("sbuf", [128, 144], "bfloat16"), "mst8": ("sbuf", [128, 144], "bfloat16"),
+    "mqa": ("sbuf", [128, 128], "bfloat16"), "mq": ("sbuf", [128, 128], "bfloat16"),
+    "hq": ("sbuf", [128, 2048], "bfloat16"),
+    "pa": ("sbuf", [128, 1024], "bfloat16"), "pb": ("sbuf", [128, 1024], "bfloat16"),
+    "vm": ("sbuf", [128, 240], "bfloat16"), "vt": ("sbuf", [128, 16], "float32"), "ve": ("sbuf", [128, 16], "float32"),
+    "rio": ("sbuf", [128, 16], "float32"), "ki": ("sbuf", [128, 8], "int32"), "kp": ("sbuf", [128, 8], "int32"),
+    "kd": ("sbuf", [128, 8], "int32"), "ks": ("sbuf", [128, 8], "int32"), "kw": ("sbuf", [128, 8], "int32"),
+    "kf": ("sbuf", [128, 8], "float32"), "indb": ("sbuf", [128, 8], "float32"), "mb": ("sbuf", [128, 8], "float32"),
+    "qm": ("sbuf", [128, 128], "bfloat16"), "qp": ("sbuf", [128, 128], "bfloat16"),
+    "dj": ("sbuf", [128, 32], "float32"),
+    "d0": ("psum", [128, 1024], "float32"), "d1": ("psum", [128, 1024], "float32"),
+    "p0": ("psum", [128, 512], "float32"), "p1": ("psum", [128, 512], "float32"),
+    "p2": ("psum", [128, 512], "float32"), "p3": ("psum", [128, 512], "float32"),
+}
+for _i in range(NAD):
+    SCRATCH["ad%d" % _i] = ("sbuf", [128, 1024], "bfloat16")
+LOADS = ["lr", "lx", "lc"]
+SEMAPHORES = (["qV", "qS", "qT", "qG"] + LOADS + ["oc"] + ["oy%d" % c for c in range(NC)]
+              + ["ar%d_%d" % (t, c) for t in range(1, RO) for c in range(NC)]
+              + ["ls%d_%d" % (t, c) for t in range(1, RO) for c in range(NC)])
+
+CYC, TCYC = 0.00083, 0.00042
+GF, SCF = 1.56, 3.8
+LAT = 0.12
+POOLS = {"D": ["d0", "d1"], "B": ["p0", "p1", "p2", "p3"]}
+
+
+def build_ops():
+    ops, tiles = [], []
+
+    def tile(pool, chain):
+        tiles.append({"pool": pool, "chain": chain, "users": 0, "buf": None})
+        return ("tile", len(tiles) - 1)
+
+    def op(qs, fn, reads, writes, dur, name="", sem=None, pos=0):
+        ops.append({"qs": qs, "fn": fn, "r": reads, "w": writes, "dur": dur, "name": name, "sem": sem, "id": len(ops)})
+        return len(ops) - 1
+
+    def R(buf, lo=0, hi=None):
+        if isinstance(buf, tuple):
+            return (buf, 0, 512)
+        return (buf, lo, SCRATCH[buf][1][1] if hi is None else hi)
+
+    def v(fn, reads, writes, cyc, name=""):
+        return op("V", fn, reads, writes, 0.055 + CYC * cyc, name)
+
+    def s(fn, reads, writes, cyc, name=""):
+        return op("S", fn, reads, writes, 0.065 + CYC * cyc, name)
+
+    def gp(fn, reads, writes, n, name=""):
+        return op("G", fn, reads, writes, 0.17 + 2 * CYC * n, name)
+
+    def mm(mats, reads, writes, name=""):
+        cols = mats[0]
+        return op("T", mats[1], reads, writes, cols * TCYC + 0.03, name)
+
+    def sel(out, in_, pat, cmp, fill, base, cm, n):
+        return gp(lambda e, B, inc: inc(e.affine_select(out=out(B), in_=in_(B), pattern=pat, compare_op=cmp, fill=fill, base=base, channel_multiplier=cm)), None, None, n)
+
+    op("A", lambda e, B, inc: inc(e.dma_start(B("r0i")[:, :], B("IN")["r0"][:, :])), [], [R("r0i")], 2.5, "load r0", sem="lr")
+    op("Y", lambda e, B, inc: inc(e.dma_start(B("xs")[:, :], B("IN")["x"][:, :])), [], [R("xs")], 5.0, "load x", sem="lx")
+    op("Y", lambda e, B, inc: inc(e.dma_start(B("c0i")[:, :], B("IN")["c0"][:, :])), [], [R("c0i")], 4.0, "load c0", sem="lc")
+
+    def fill(buf, val, n, lo=0):
+        v(lambda e, B, inc: inc(e.memset(B(buf)[:, lo:lo + n], val)), [], [R(buf, lo, lo + n)], n / 2)
+
+    def gsel(dst, src, pat, cmp, fillv, base, cm, n):
+        gp(lambda e, B, inc: inc(e.affine_select(out=B(dst)[:, 0:n], in_=B(src)[:, 0:n], pattern=pat, compare_op=cmp, fill=fillv, base=base, channel_multiplier=cm)),
+           [R(src, 0, n)], [R(dst, 0, n)], n, "sel " + dst)
+
+    def scale(dst, src, k):
+        n = SCRATCH[src][1][1]
+        v(lambda e, B, inc: inc(e.tensor_scalar(out=B(dst)[:, 0:n], in0=B(src)[:, 0:n], scalar1=float(k), scalar2=None, op0=A.mult)),
+          [R(src)], [R(dst)], n / 2)
+
+    def addm(dst, a, b):
+        v(lambda e, B, inc: inc(e.tensor_tensor(out=B(dst)[:, 0:128], in0=B(a)[:, 0:128], in1=B(b)[:, 0:128], op=A.add)), [R(a), R(b)], [R(dst)], 256)
+
+    fill("ones", 1.0, 2048)
+    gsel("ey", "ones", [[-1, 128]], A.is_equal, 0.0, 0, 1, 128)
+    gsel("b8a", "ones", [[-16, 8]], A.is_ge, 0.0, 0, 1, 8)
+    gsel("b8", "b8a", [[16, 8]], A.is_ge, 0.0, 15, -1, 8)
+    gsel("b15", "ones", [[-16, 8]], A.is_equal, 0.0, -15, 1, 8)
+    scale("ney", "ey", -1)
+    fill("mst", 0.0, 144)
+    fill("mst15", 0.0, 144)
+    for d_, s_ in (("mst", "b8"), ("mst15", "b15")):
+        v(lambda e, B, inc, d_=d_, s_=s_: inc(e.tensor_copy(out=B(d_)[:, 15:143:16], in_=B(s_)[:, 0:8])), [R(s_)], [R(d_)], 64)
+    gsel("bo1", "ones", [[-16, 8], [0, 16]], A.is_ge, 0.0, 0, 1, 128)
+    gsel("bo", "bo1", [[16, 8], [0, 16]], A.is_ge, 0.0, 15, -1, 128)
+    gsel("ux", "bo", [[1, 128]], A.is_gt, 0.0, 0, -1, 128)
+    scale("ux8", "ux", -8)
+    gsel("wq", "ux8", [[-1, 128]], A.not_equal, 0.5, 0, 1, 128)
+    gsel("u15", "ux", [[0, 8], [-1, 16]], A.is_gt, 0.0, 15, 0, 128)
+    scale("u15s", "u15", -SH)
+    scale("u15n", "u15", -1)
+    gp(lambda e, B, inc: inc(e.iota(B("ki")[:, 0:1], [[0, 1]], 0, 1)), [], [R("ki")], 8)
+    gp(lambda e, B, inc: inc(e.iota(B("rio")[:, 0:16], [[1, 16]], 0, 0, allow_small_or_imprecise_dtypes=True)), [], [R("rio")], 16)
+    gp(lambda e, B, inc: inc(e.iota(B("dj")[:, 0:32], [[16, 32]], H, 0, allow_small_or_imprecise_dtypes=True)), [], [R("dj")], 32)
+    ts = lambda dst, src, s1, o1, s2=None, o2=None, n=1: v(
+        (lambda e, B, inc: inc(e.tensor_scalar(out=B(dst)[:, 0:n], in0=B(src)[:, 0:n], scalar1=s1, scalar2=None, op0=o1))) if o2 is None else
+        (lambda e, B, inc: inc(e.tensor_scalar(out=B(dst)[:, 0:n], in0=B(src)[:, 0:n], scalar1=s1, scalar2=s2, op0=o1, op1=o2))), [R(src)], [R(dst)], 64)
+    ts("kp", "ki", 15, A.bitwise_and)
+    ts("indb", "kp", -8.0, A.mult, 0.5, A.add)
+    ts("mb", "kp", 16.0, A.mult, -17.0, A.add)
+    ts("kd", "ki", 4, A.arith_shift_right)
+    v(lambda e, B, inc: inc(e.tensor_tensor(out=B("ks")[:, 0:1], in0=B("kp")[:, 0:1], in1=B("kd")[:, 0:1], op=A.add)), [R("kp"), R("kd")], [R("ks")], 64)
+    ts("kw", "ks", 1.0, A.add)
+    v(lambda e, B, inc: inc(e.tensor_scalar(out=B("ks")[:, 2:3], in0=B("kw")[:, 0:1], scalar1=15, scalar2=None, op0=A.bitwise_and)), [R("kw")], [R("ks")], 64)
+    v(lambda e, B, inc: inc(e.tensor_tensor(out=B("kf")[:, 0:1], in0=B("kp")[:, 0:1], in1=B("ks")[:, 2:3], op=A.min)), [R("kp"), R("ks")], [R("kf")], 64)
+    v(lambda e, B, inc: inc(e.tensor_copy(out=B("kf")[:, 1:2], in_=B("kp")[:, 0:1])), [R("kp")], [R("kf", 1, 2)], 64)
+    v(lambda e, B, inc: inc(e.tensor_scalar(out=B("dj")[:, 0:32], in0=B("dj")[:, 0:32], scalar1=B("kf")[:, 1:2], scalar2=None, op0=A.add)), [R("dj"), R("kf")], [R("dj")], 64)
+    fill("vm", 0.0, 240)
+    v(lambda e, B, inc: inc(e.tensor_scalar(out=B("vt")[:, 0:16], in0=B("rio")[:, 0:16], scalar1=B("kf")[:, 0:1], scalar2=-100.0, op0=A.is_gt, op1=A.mult)), [R("rio"), R("kf")], [R("vt")], 64)
+    v(lambda e, B, inc: inc(e.tensor_scalar(out=B("ve")[:, 0:16], in0=B("rio")[:, 0:16], scalar1=B("kf")[:, 0:1], scalar2=None, op0=A.is_equal)), [R("rio"), R("kf")], [R("ve")], 64)
+    v(lambda e, B, inc: inc(e.tensor_tensor(out=B("vm")[:, 112:128], in0=B("vt")[:, 0:16], in1=B("ve")[:, 0:16], op=A.add)), [R("vt"), R("ve")], [R("vm")], 64)
+    fill("pa", 0.0, 1024)
+    gsel("pb", "pa", [[-16, 8], [0, 8], [-1, 16]], A.not_equal, 1.0, 0, 1, 1024)
+    gsel("pa", "pb", [[-16, 8], [-1, 8], [-1, 16]], A.not_equal, -1.0, -1, 1, 1024)
+    gsel("pb", "pa", [[-16, 8], [-1, 8], [-1, 16]], A.not_equal, -1.0, 15, 1, 1024)
+    gsel("pa", "pb", [[-16, 8], [0, 128]], A.is_ge, 0.0, 0, 1, 1024)
+    gsel("pb", "pa", [[16, 8], [0, 128]], A.is_ge, 0.0, 15, -1, 1024)
+    scale("boq", "bo", 0.25)
+    scale("hey", "ey", 0.5)
+    addm("boqp", "boq", "hey")
+    v(lambda e, B, inc: inc(e.tensor_tensor(out=B("boqm")[:, 0:128], in0=B("boq")[:, 0:128], in1=B("hey")[:, 0:128], op=A.subtract)), [R("boq"), R("hey")], [R("boqm")], 256)
+    gsel("tl", "bo", [[-1, 128]], A.is_ge, 0.0, 0, 1, 128)
+    scale("tl2", "tl", 2)
+    gsel("au", "bo", [[1, 128]], A.is_ge, 0.0, 0, -1, 128)
+    scale("au16", "au", 16)
+    gsel("hq", "ones", [[-1, 16], [-16, 8], [0, 16]], A.is_equal, 0.0, 0, 1, 2048)
+    gsel("mqa", "ones", [[0, 16], [-16, 8]], A.is_ge, 0.0, 0, 1, 128)
+    gsel("mq", "mqa", [[1, 16], [16, 8]], A.is_ge, 0.0, -1, -1, 128)
+    gsel("mst8", "ones", [[-1, 144]], A.is_equal, 0.0, 15, 16, 144)
+    fill("qm", 0.0, 128)
+    gp(lambda e, B, inc: inc(e.affine_select(out=B("qm")[:, 1:128:2], in_=B("qm")[:, 1:128:2], pattern=[[-2, 64]], compare_op=A.not_equal, fill=0.5, base=0, channel_multiplier=1)), [R("qm")], [R("qm")], 64)
+    gp(lambda e, B, inc: inc(e.affine_select(out=B("qm")[:, 1:128:2], in_=B("qm")[:, 1:128:2], pattern=[[-2, 64]], compare_op=A.not_equal, fill=-0.5, base=-1, channel_multiplier=1)), [R("qm")], [R("qm")], 64)
+    v(lambda e, B, inc: inc(e.memset(B("qm")[:, 15:128:16], 0.0)), [], [R("qm")], 64)
+    addm("qp", "qm", "ey")
+    fill("c1536", float(SH), CH)
+    fill("onesf", 1.0, 128)
+    fill("zero", 0.0, 8)
+    fill("cache", 0.0, P, H)
+    v(lambda e, B, inc: inc(e.tensor_copy(out=B("cache")[:, 0:H], in_=B("c0i")[:, :])), [R("c0i")], [R("cache", 0, H)], H)
+
+    adn = [0]
+
+    def E(B, p, m="mst"):
+        return B(m)[:, 15 - p:143 - p]
+
+    def dist(vb, c, pairs, chain):
+        ds = tile("B", chain)
+        lo, hi = 16 * c * CH, 16 * (c + 1) * CH
+        for i0 in range(0, len(pairs), RT):
+            part = pairs[i0:i0 + RT]
+            d = tile("D", chain + "d")
+            ad = "ad%d" % (adn[0] % NAD)
+            adn[0] += 1
+
+            def diff(e, B, inc, part=part, d=d):
+                for i, (p, p2, row) in enumerate(part):
+                    o = B(d)[:, i * CH:(i + 1) * CH]
+                    inc(e.matmul(o, B("ey")[:, :], B(vb)[:, lo + p:hi:16], True, False))
+                    inc(e.matmul(o, B("ney")[:, :], B(vb)[:, lo + p2:hi:16], False, True))
+            mm((2 * CH * len(part), diff), [R(vb, lo, hi), R("ey"), R("ney")], [R(d)], "diff")
+            w = CH * len(part)
+            s(lambda e, B, inc, d=d, ad=ad, w=w: inc(e.activation(B(ad)[:, 0:w], B(d)[:, 0:w], F.Abs)), [R(d)], [R(ad)], w, "abs")
+
+            def summ(e, B, inc, part=part, ad=ad, i0=i0):
+                for i, (p, p2, row) in enumerate(part):
+                    inc(e.matmul(B(ds)[:, 0:CH], E(B, row), B(ad)[:, i * CH:(i + 1) * CH], i0 + i == 0, i0 + i == len(pairs) - 1))
+            mm((CH * len(part), summ), [R(ad), R("mst")], [R(ds)], "sum")
+        return ds
+
+    def gather(vb, off, c):
+        for j in range(c * CH, (c + 1) * CH, KG):
+            def fn(e, B, inc, j=j, q=None):
+                o, w = B(vb)[:, 16 * j:16 * (j + KG)], B("xs")[:, 0:W].indirect(B(off)[:, j:j + KG])
+                if B("Q") == "V":
+                    inc(e.tensor_copy(out=o, in_=w))
+                else:
+                    inc(e.activation(o, w, F.Copy))
+            op("VS", fn, [R("xs"), R(off, j, j + KG)], [R(vb, 16 * j, 16 * (j + KG))], 0.06 + GF * CYC * 16 * KG, "gather")
+
+    def first_fail(ds, c, sbuf, ibuf, chain):
+        j0, j1 = c * CH, (c + 1) * CH
+        s(lambda e, B, inc: inc(e.activation(B(sbuf)[:, j0:j1], B(ds)[:, 0:CH], F.Sign, bias=B("kf")[:, 2:3])), [R(ds), R("kf")], [R(sbuf, j0, j1)], CH, "bad")
+        qt = tile("B", chain)
+        mm((CH, lambda e, B, inc: inc(e.matmul(B(qt)[:, 0:CH], B("wq")[:, :], B(sbuf)[:, j0:j1], True, True))), [R("wq"), R(sbuf, j0, j1)], [R(qt)], "q")
+
+        def fn(e, B, inc):
+            if B("Q") == "S":
+                inc(e.activation(B(ibuf)[:, j0:j1], B(qt)[:, 0:CH], F.Relu, bias=B("indb")[:, 0:1]))
+            else:
+                inc(e.tensor_scalar(out=B(ibuf)[:, j0:j1], in0=B(qt)[:, 0:CH], scalar1=B("indb")[:, 0:1], scalar2=0.0, op0=A.add, op1=A.max))
+        op("SV", fn, [R(qt), R("indb")], [R(ibuf, j0, j1)], 0.06 + CYC * CH, "ind")
+
+    for i, val in ((2, -40.5), (3, 40.5), (4, -0.5)):
+        v(lambda e, B, inc, i=i, val=val: inc(e.memset(B("kf")[:, i:i + 1], val)), [], [R("kf", i, i + 1)], 64)
+
+    def phase_a(t, c):
+        j0, j1 = c * CH, (c + 1) * CH
+        rf = "rf%d" % t
+        if t == 0:
+            v(lambda e, B, inc: inc(e.tensor_copy(out=B("ru")[:, j0:j1], in_=B("r0i")[:, j0:j1])), [R("r0i", j0, j1)], [R("ru", j0, j1)], CH, "ru")
+            v(lambda e, B, inc: inc(e.tensor_scalar(out=B(rf)[:, j0:j1], in0=B("r0i")[:, j0:j1], scalar1=float(-SH), scalar2=None, op0=A.add)), [R("r0i", j0, j1)], [R(rf, j0, j1)], CH, "rf")
+        else:
+            v(lambda e, B, inc: inc(e.tensor_scalar(out=B("ru")[:, j0:j1], in0=B(rf)[:, j0:j1], scalar1=float(SH), scalar2=None, op0=A.add)), [R(rf, j0, j1)], [R("ru", j0, j1)], CH / 2, "ru")
+        gather("va", "ru", c)
+        ch = "A%d_%d" % (t, c)
+        l15 = tile("B", ch + "r")
+
+        def f15(e, B, inc):
+            for q in range(16):
+                inc(e.matmul(B(l15)[:, 0:NL], E(B, q, "mst15"), B(rf)[:, j0 + q:j1:16], q == 0, q == 15))
+        mm((16 * 64, f15), [R("mst15"), R(rf, j0, j1)], [R(l15)], "r15")
+        v(lambda e, B, inc: inc(e.tensor_scalar(out=B("r15")[:, c * NL:(c + 1) * NL], in0=B(l15)[:, 0:NL], scalar1=float(SH), scalar2=None, op0=A.add)),
+          [R(l15)], [R("r15", c * NL, (c + 1) * NL)], 64, "r15")
+        ds = dist("va", c, [(p, p + 1, p) for p in range(15)], ch)
+        first_fail(ds, c, "sb", "ind", ch)
+
+    def phase_b(t, c):
+        j0, j1, k0, k1 = c * CH, (c + 1) * CH, c * NL, (c + 1) * NL
+        rf, ch = "rf%d" % t, "B%d_%d" % (t, c)
+        wm = tile("B", ch)
+
+        def fwm(e, B, inc):
+            inc(e.matmul(B(wm)[:, 0:CH], B("ey")[:, :], B(rf)[:, j0:j1], True, False))
+            inc(e.matmul(B(wm)[:, 0:CH], B("u15s")[:, :], B("ind")[:, j0:j1], False, True))
+            inc(e.matmul(B(wm)[:, CH:2 * CH], B("u15")[:, :], B("ind")[:, j0:j1], True, True))
+        mm((3 * CH, fwm), [R("ey"), R("u15"), R("u15s"), R(rf, j0, j1), R("ind", j0, j1)], [R(wm)], "wm")
+        v(lambda e, B, inc: inc(e.tensor_tensor(out=B("indr")[:, j0:j1], in0=B(wm)[:, 0:CH], in1=B("ind")[:, j0:j1], op=A.mult)), [R(wm), R("ind", j0, j1)], [R("indr", j0, j1)], CH, "indr")
+        ll = tile("B", ch)
+
+        def ffl(e, B, inc):
+            for q in range(16):
+                inc(e.matmul(B(ll)[:, NL:2 * NL], E(B, q), B("ind")[:, j0 + q:j1:16], q == 0, q == 15))
+        mm((16 * 64, ffl), [R("mst"), R("ind", j0, j1)], [R(ll)], "fail list")
+
+        def frk(e, B, inc):
+            for q in range(16):
+                inc(e.matmul(B(ll)[:, 0:NL], E(B, q), B("indr")[:, j0 + q:j1:16], q == 0, q == 15))
+        mm((16 * 64, frk), [R("mst"), R("indr", j0, j1)], [R(ll)], "rk list")
+        lst = lambda b: B_(b)
+        v(lambda e, B, inc: inc(e.tensor_scalar(out=B("rk")[:, k0:k1], in0=B(ll)[:, 0:NL], scalar1=float(SH), scalar2=None, op0=A.add)), [R(ll)], [R("rk", k0, k1)], 64, "l")
+        v(lambda e, B, inc: inc(e.tensor_tensor(out=B("pri")[:, k0:k1], in0=B("rk")[:, k0:k1], in1=B("r15")[:, k0:k1], op=A.mult)), [R("rk", k0, k1), R("r15", k0, k1)], [R("pri", k0, k1)], 64, "l")
+        if t == 0:
+            rkk = "rk"
+        else:
+            rkk = "rkk"
+            v(lambda e, B, inc: inc(e.tensor_scalar(out=B("rkk")[:, k0:k1], in0=B(ll)[:, 0:NL], scalar1=float(SH), scalar2=B("kcol")[:, t:t + 1], op0=A.add, op1=A.add)), [R(ll), R("kcol", t, t + 1)], [R("rkk", k0, k1)], 64, "l")
+        v(lambda e, B, inc: inc(e.tensor_scalar(out=B("nfl")[:, k0:k1], in0=B(ll)[:, NL:2 * NL], scalar1=-1.0, scalar2=1.0, op0=A.mult, op1=A.add)), [R(ll)], [R("nfl", k0, k1)], 64, "l")
+        v(lambda e, B, inc: inc(e.tensor_tensor(out=B("djn")[:, k0:k1], in0=B("nfl")[:, k0:k1], in1=B("dj")[:, k0:k1], op=A.mult)), [R("nfl", k0, k1), R("dj")], [R("djn", k0, k1)], 64, "l")
+        v(lambda e, B, inc: inc(e.tensor_scalar(out=B("fi")[:, k0:k1], in0=B("pri")[:, k0:k1], scalar1=6, scalar2=None, op0=A.arith_shift_right)), [R("pri", k0, k1)], [R("fi", k0, k1)], 64, "l")
+        v(lambda e, B, inc: inc(e.tensor_tensor(out=B("si")[:, k0:k1], in0=B("fi")[:, k0:k1], in1=B(rkk)[:, k0:k1], op=A.add)), [R("fi", k0, k1), R(rkk, k0, k1)], [R("si", k0, k1)], 64, "l")
+        v(lambda e, B, inc: inc(e.tensor_scalar(out=B("hm")[:, k0:k1], in0=B("si")[:, k0:k1], scalar1=H - 1, scalar2=None, op0=A.bitwise_and)), [R("si", k0, k1)], [R("hm", k0, k1)], 64, "l")
+        v(lambda e, B, inc: inc(e.tensor_tensor(out=B("hf")[:, k0:k1], in0=B("hm")[:, k0:k1], in1=B("djn")[:, k0:k1], op=A.max)), [R("hm", k0, k1), R("djn", k0, k1)], [R("hf", k0, k1)], 64, "l")
+        v(lambda e, B, inc: inc(e.tensor_copy(out=B("hu")[:, k0:k1], in_=B("hf")[:, k0:k1])), [R("hf", k0, k1)], [R("hu", k0, k1)], 64, "hu")
+        v(lambda e, B, inc: inc(e.tensor_tensor(out=B("t1")[:, j0:j1], in0=B("cache")[:, 0:H + P].indirect(B("hu")[:, k0:k1]), in1=B(rf)[:, j0:j1], op=A.subtract)),
+          [R("cache"), R("hu", k0, k1), R(rf, j0, j1)], [R("t1", j0, j1)], GF * CH, "cache gather")
+        v(lambda e, B, inc: inc(e.tensor_tensor(out=B("t2")[:, j0:j1], in0=B(wm)[:, CH:2 * CH], in1=B("t1")[:, j0:j1], op=A.mult)), [R(wm), R("t1", j0, j1)], [R("t2", j0, j1)], CH, "t2")
+        v(lambda e, B, inc: inc(e.tensor_tensor(out=B("r2")[:, j0:j1], in0=B(wm)[:, 0:CH], in1=B("t2")[:, j0:j1], op=A.add)), [R(wm), R("t2", j0, j1)], [R("r2", j0, j1)], CH, "r2")
+        gpt = 1024 // CH
+        b0 = c * 2048
+        for g0 in range(0, 8, gpt):
+            d = tile("D", ch + "p")
+
+            def fpr(e, B, inc, d=d, g0=g0):
+                for i in range(gpt):
+                    inc(e.matmul(B(d)[:, i * CH:(i + 1) * CH], B("pb")[:, 128 * (g0 + i):128 * (g0 + i + 1)], B("r2")[:, j0:j1], True, True))
+            mm((gpt * CH, fpr), [R("pb"), R("r2", j0, j1)], [R(d)], "pairs")
+            v(lambda e, B, inc, d=d, g0=g0: inc(e.tensor_scalar(out=B("eqp")[:, b0 + g0 * CH:b0 + (g0 + gpt) * CH], in0=B(d)[:, 0:gpt * CH], scalar1=0.0, scalar2=None, op0=A.is_equal)),
+              [R(d)], [R("eqp", b0 + g0 * CH, b0 + (g0 + gpt) * CH)], gpt * CH, "eq")
+        vt = tile("B", ch)
+
+        def fv(e, B, inc):
+            for g in range(8):
+                inc(e.matmul(B(vt)[:, 0:CH], B("vm")[:, 112 - 16 * g:240 - 16 * g], B("eqp")[:, b0 + g * CH:b0 + (g + 1) * CH], g == 0, g == 7))
+        mm((8 * CH, fv), [R("vm"), R("eqp", b0, b0 + 8 * CH)], [R(vt)], "V")
+        s(lambda e, B, inc: inc(e.activation(B("sf")[:, j0:j1], B(vt)[:, 0:CH], F.Sign, bias=B("kf")[:, 4:5])), [R(vt), R("kf")], [R("sf", j0, j1)], CH, "f")
+        rc = tile("B", ch)
+        mm((CH, lambda e, B, inc: inc(e.matmul(B(rc)[:, 0:CH], B("ey")[:, :], B("r2")[:, j0:j1], True, True))), [R("ey"), R("r2", j0, j1)], [R(rc)], "copy r2")
+        v(lambda e, B, inc: inc(e.tensor_tensor(out=B("fr")[:, j0:j1], in0=B(rc)[:, 0:CH], in1=B("sf")[:, j0:j1], op=A.mult)), [R(rc), R("sf", j0, j1)], [R("fr", j0, j1)], CH, "fr")
+        xm = tile("B", ch)
+
+        def fxm(e, B, inc):
+            inc(e.matmul(B(xm)[:, 0:CH], B("boqm")[:, :], B("r2")[:, j0:j1], True, False))
+            inc(e.matmul(B(xm)[:, 0:CH], B("boq")[:, :], B("fr")[:, j0:j1], False, True))
+        mm((2 * CH, fxm), [R("boqm"), R("boq"), R("r2", j0, j1), R("fr", j0, j1)], [R(xm)], "xm")
+        v(lambda e, B, inc: inc(e.tensor_scalar(out=B("ee")[:, j0:j1], in0=B(xm)[:, 0:CH], scalar1=0.0, scalar2=None, op0=A.is_equal)), [R(xm)], [R("ee", j0, j1)], CH, "E")
+        v2 = tile("B", ch)
+
+        def fv2(e, B, inc):
+            inc(e.matmul(B(v2)[:, 0:CH], B("au16")[:, :], B("sf")[:, j0:j1], True, False))
+            inc(e.matmul(B(v2)[:, 0:CH], B("tl2")[:, :], B("ee")[:, j0:j1], False, True))
+        mm((2 * CH, fv2), [R("au16"), R("tl2"), R("sf", j0, j1), R("ee", j0, j1)], [R(v2)], "v2")
+        s(lambda e, B, inc: inc(e.activation(B("sm")[:, j0:j1], B(v2)[:, 0:CH], F.Sign, bias=B("mb")[:, 0:1])), [R(v2), R("mb")], [R("sm", j0, j1)], CH, "M")
+        v(lambda e, B, inc: inc(e.tensor_tensor(out=B("t3")[:, j0:j1], in0=B(xm)[:, 0:CH], in1=B("sm")[:, j0:j1], op=A.mult)), [R(xm), R("sm", j0, j1)], [R("t3", j0, j1)], CH, "t3")
+        xp = tile("B", ch)
+
+        def fxp(e, B, inc):
+            inc(e.matmul(B(xp)[:, 0:CH], B("boqp")[:, :], B("r2")[:, j0:j1], True, False))
+            inc(e.matmul(B(xp)[:, 0:CH], B("boq")[:, :], B("fr")[:, j0:j1], False, True))
+        mm((2 * CH, fxp), [R("boqp"), R("boq"), R("r2", j0, j1), R("fr", j0, j1), R("sm", j0, j1)], [R(xp)], "xp")
+        v(lambda e, B, inc: inc(e.tensor_tensor(out=B("rp")[:, j0:j1], in0=B(xp)[:, 0:CH], in1=B("t3")[:, j0:j1], op=A.add)), [R(xp), R("t3", j0, j1)], [R("rp", j0, j1)], CH, "rp")
+        v(lambda e, B, inc: inc(e.tensor_scalar(out=B("rpu")[:, j0:j1], in0=B("rp")[:, j0:j1], scalar1=float(SH), scalar2=None, op0=A.add)), [R("rp", j0, j1)], [R("rpu", j0, j1)], CH / 2, "rpu")
+
+    def hrep(t, c):
+        j0, j1, k0, k1 = c * CH, (c + 1) * CH, c * NL, (c + 1) * NL
+        v(lambda e, B, inc: inc(e.tensor_copy(out=B("hh")[:, k0:k1], in_=B("hf")[:, k0:k1])), [R("hf", k0, k1)], [R("hh", k0, k1)], 64, "hh")
+        hr = tile("B", "H%d_%d" % (t, c))
+
+        def fh(e, B, inc):
+            for q in range(16):
+                inc(e.matmul(B(hr)[:, q:CH:16], B("hq")[:, 128 * q:128 * (q + 1)], B("hh")[:, k0:k1], True, True))
+        mm((16 * 64, fh), [R("hq"), R("hh", k0, k1)], [R(hr)], "hrep")
+        v(lambda e, B, inc: inc(e.tensor_copy(out=B("hrep")[:, j0:j1], in_=B(hr)[:, 0:CH])), [R(hr)], [R("hrep", j0, j1)], CH, "hrep")
+
+    def winners(t):
+        if t < RO - 1:
+            v(lambda e, B, inc: inc(e.tensor_reduce(out=B("ksum")[:, t:t + 1], in_=B("nfl")[:, 0:32], axis=AxisListType.X, op=A.add)), [R("nfl")], [R("ksum", t, t + 1)], 64, "K")
+            kt = tile("B", "K%d" % t)
+            mm((256, lambda e, B, inc: inc(e.matmul(B(kt)[:, 0:1], B("onesf")[:, :], B("ksum")[:, t:t + 1], True, True))), [R("onesf"), R("ksum", t, t + 1)], [R(kt)], "K")
+            v(lambda e, B, inc: inc(e.tensor_scalar(out=B("kcol")[:, t + 1:t + 2], in0=B(kt)[:, 0:1], scalar1=-1.0, scalar2=float(8 * P), op0=A.mult, op1=A.add)), [R(kt)], [R("kcol", t + 1, t + 2)], 64, "K")
+        for k in range(32):
+            n = P - 16 * k
+            v(lambda e, B, inc, k=k, n=n: inc(e.tensor_scalar(out=B("eqw")[:, P * k:P * k + n], in0=B("hrep")[:, 16 * k:P], scalar1=B("hf")[:, k:k + 1], scalar2=None, op0=A.is_equal)),
+              [R("hrep", 16 * k, P), R("hf", k, k + 1)], [R("eqw", P * k, P * k + n)], n / 2, "win")
+        z = tile("B", "W%d" % t)
+        for k0 in range(0, 32, 4):
+            def fz(e, B, inc, k0=k0):
+                if k0 == 0:
+                    inc(e.matmul(B(z)[0:8, 0:P], B("zero")[:, 0:8], B("eqw")[:, 0:P], True, False))
+                for k in range(k0, min(k0 + 4, 31)):
+                    inc(e.matmul(B(z)[0:8, 16 * (k + 1):P], B("b8")[:, 0:8], B("eqw")[:, P * k + 16:P * k + P - 16 * k], False, False))
+            mm((4 * (P - 16 * k0), fz), [R("zero"), R("b8"), R("eqw", P * k0, P * (k0 + 3) + P - 16 * (k0 + 3))], [R(z)], "Z")
+
+        def fzd(e, B, inc):
+            for q in range(16):
+                inc(e.matmul(B(z)[0:8, q:P:16], B("mq")[:, 8 * q:8 * q + 8], B("eqw")[:, q:32 * P:P], False, q == 15))
+        mm((16 * 32, fzd), [R("mq"), R("eqw")], [R(z)], "Zd")
+        s(lambda e, B, inc: inc(e.activation(B("lose")[0:8, 0:P], B(z)[0:8, 0:P], F.Sign)), [R(z)], [R("lose")], P, "lose")
+        wl = tile("B", "W%d" % t)
+
+        def fl(e, B, inc):
+            for q in range(16):
+                inc(e.matmul(B(wl)[:, 0:32], B("mst8")[0:8, 15 - q:143 - q], B("lose")[0:8, q:P:16], q == 0, q == 15))
+        mm((16 * 64, fl), [R("mst8"), R("lose")], [R(wl)], "lose list")
+        v(lambda e, B, inc: inc(e.tensor_tensor(out=B("lt")[:, 0:32], in0=B(wl)[:, 0:32], in1=B("dj")[:, 0:32], op=A.mult)), [R(wl), R("dj")], [R("lt")], 64, "w")
+        v(lambda e, B, inc: inc(e.tensor_tensor(out=B("lo")[:, 0:32], in0=B("lt")[:, 0:32], in1=B("hf")[:, 0:32], op=A.max)), [R("lt"), R("hf")], [R("lo")], 64, "w")
+        v(lambda e, B, inc: inc(e.tensor_copy(out=B("wu")[:, 0:32], in_=B("lo")[:, 0:32])), [R("lo")], [R("wu")], 64, "w")
+
+    def phase_d(t, c):
+        ch = "D%d_%d" % (t, c)
+        gather("vd", "rpu", c)
+        ds = dist("vd", c, [(p, p + 1, p) for p in range(15)], ch)
+        first_fail(ds, c, "sb2", "ind2", ch)
+        return dist("vd", c, [(p, p + 2, p + 1) for p in range(0, 14, 2)], ch + "n")
+
+    def phase_e(t, c, dn):
+        j0, j1 = c * CH, (c + 1) * CH
+        ch = "E%d_%d" % (t, c)
+        s(lambda e, B, inc: inc(e.activation(B("sn")[:, j0:j1], B(dn)[:, 0:CH], F.Sign, scale=-1.0, bias=B("kf")[:, 3:4])), [R(dn), R("kf")], [R("sn", j0, j1)], CH, "near")
+        n1 = tile("B", ch + "n")
+
+        def f6(e, B, inc):
+            inc(e.matmul(B(n1)[:, 0:CH], B("qm")[:, :], B("rp")[:, j0:j1], True, True))
+            if t == RO - 1:
+                inc(e.matmul(B(n1)[:, CH:2 * CH], B("qp")[:, :], B("rp")[:, j0:j1], True, False))
+                inc(e.matmul(B(n1)[:, CH:2 * CH], B("ey")[:, :], B("c1536")[:, :], False, True))
+            else:
+                inc(e.matmul(B(n1)[:, CH:2 * CH], B("qp")[:, :], B("rp")[:, j0:j1], True, True))
+        mm((2 * CH, f6), [R("qm"), R("qp"), R("ey"), R("c1536"), R("rp", j0, j1), R("sn", j0, j1)], [R(n1)], "n1")
+        v(lambda e, B, inc: inc(e.tensor_tensor(out=B("t5")[:, j0:j1], in0=B(n1)[:, 0:CH], in1=B("sn")[:, j0:j1], op=A.mult)), [R(n1), R("sn", j0, j1)], [R("t5", j0, j1)], CH, "t5")
+        out = "yrs" if t == RO - 1 else "rn%d" % t
+        v(lambda e, B, inc: inc(e.tensor_tensor(out=B(out)[:, j0:j1], in0=B(n1)[:, CH:2 * CH], in1=B("t5")[:, j0:j1], op=A.add)), [R(n1), R("t5", j0, j1)], [R(out, j0, j1)], CH, "rn")
+        if t == RO - 1:
+            op("Y", lambda e, B, inc: inc(e.dma_start(B("IN")["yr"][:, j0:j1], B("yrs")[:, j0:j1])), [R("yrs", j0, j1)], [("yr", j0, j1)], 2.5, "store yr", sem="oy%d" % c)
+        else:
+            op("G", ("send", t, c, j0, j1), [R(out, j0, j1)], [], 1.0, "send", sem="ls%d_%d" % (t + 1, c))
+            ops[-1]["sem2"] = "ar%d_%d" % (t + 1, c)
+            op("N", ("arrive", t + 1, c), [R(out, j0, j1)], [R("rf%d" % (t + 1), j0, j1)], 3.5, "arrive", sem="ar%d_%d" % (t + 1, c))
+            ops[-1]["after"] = len(ops) - 2
+        om = tile("B", ch)
+
+        def fom(e, B, inc):
+            inc(e.matmul(B(om)[:, 0:CH], B("ey")[:, :], B("ones")[:, 0:CH], True, False))
+            inc(e.matmul(B(om)[:, 0:CH], B("u15n")[:, :], B("ind2")[:, j0:j1], False, True))
+            inc(e.matmul(B(om)[:, CH:2 * CH], B("ey")[:, :], B("rp")[:, j0:j1], True, True))
+        mm((3 * CH, fom), [R("ey"), R("ones"), R("u15n"), R("ind2", j0, j1), R("rp", j0, j1)], [R(om)], "om")
+        v(lambda e, B, inc: inc(e.tensor_tensor(out=B("indr2")[:, j0:j1], in0=B(om)[:, CH:2 * CH], in1=B("ind2")[:, j0:j1], op=A.mult)), [R(om), R("ind2", j0, j1)], [R("indr2", j0, j1)], CH, "indr2")
+        v(lambda e, B, inc: inc(e.tensor_tensor(out=B("t4")[:, j0:j1], in0=B(om)[:, 0:CH], in1=B("rp")[:, j0:j1], op=A.mult)), [R(om), R("rp", j0, j1)], [R("t4", j0, j1)], CH, "t4")
+        sk = tile("B", ch)
+
+        def fsk(e, B, inc):
+            inc(e.matmul(B(sk)[:, 0:CH], B("ey")[:, :], B("c1536")[:, :], True, False))
+            inc(e.matmul(B(sk)[:, 0:CH], B("u15")[:, :], B("indr2")[:, j0:j1], False, True))
+        mm((2 * CH, fsk), [R("ey"), R("c1536"), R("u15"), R("indr2", j0, j1)], [R(sk)], "sk")
+        v(lambda e, B, inc: inc(e.tensor_tensor(out=B("st")[:, j0:j1], in0=B(sk)[:, 0:CH], in1=B("t4")[:, j0:j1], op=A.add)), [R(sk), R("t4", j0, j1)], [R("st", j0, j1)], CH, "st")
+
+    for t in range(RO):
+        for c in range(NC):
+            phase_a(t, c)
+        for c in range(NC):
+            phase_b(t, c)
+            hrep(t, c)
+        winners(t)
+        for c in range(NC):
+            dn = phase_d(t, c)
+            phase_e(t, c, dn)
+        v(lambda e, B, inc: inc(e.tensor_copy(out=B("cache")[:, 0:H + P].indirect(B("wu")[:, 0:32]), in_=B("st")[:, :])), [R("wu"), R("st")], [R("cache")], SCF * P, "scatter")
+    op("Y", lambda e, B, inc: inc(e.dma_start(B("IN")["yc"][:, :], B("cache")[:, 0:H])), [R("cache", 0, H)], [("yc", 0, H)], 3.0, "store yc", sem="oc")
+    return ops, tiles
+
+
+def deps_of(ops, key, cross):
+    hist = {}
+    out = []
+    for o in ops:
+        d = {}
+        for rw, regs in (("r", o["r"]), ("w", o["w"])):
+            for (b, lo, hi) in regs:
+                for (lo2, hi2, rw2, o2) in hist.get(key(b), ()):
+                    if o2 is o or lo2 >= hi or hi2 <= lo:
+                        continue
+                    kind = rw2 + rw
+                    if kind == "rr" and not (cross(b) and o2["q"] != o["q"]):
+                        continue
+                    d.setdefault(o2["id"], set()).add((kind, cross(b)))
+        if "after" in o:
+            d.setdefault(o["after"], set()).add(("wr", False))
+        for rw, regs in (("r", o["r"]), ("w", o["w"])):
+            for (b, lo, hi) in regs:
+                h = hist.setdefault(key(b), [])
+                if rw == "w" and not cross(b):
+                    h[:] = [x for x in h if not (lo <= x[0] and x[1] <= hi)]
+                h.append((lo, hi, rw, o))
+        out.append(d)
+    return out
+
+
+def is_tile(b):
+    return isinstance(b, tuple) or b in ("d0", "d1", "p0", "p1", "p2", "p3")
+
+
+def schedule():
+    ops, tiles = build_ops()
+    for o in ops:
+        o["q"] = o["qs"][0]
+        for b, lo, hi in o["r"] + o["w"]:
+            if isinstance(b, tuple):
+                tiles[b[1]]["users"] += 1
+    dep = deps_of(ops, lambda b: b, is_tile)
+    n = len(ops)
+    succ = [[] for _ in range(n)]
+    left = [0] * n
+    for i in range(n):
+        left[i] = len(dep[i])
+        for d in dep[i]:
+            succ[d].append(i)
+    rank = [0.0] * n
+    for i in range(n - 1, -1, -1):
+        rank[i] = ops[i]["dur"] + max([rank[j] + LAT for j in succ[i]] or [0.0])
+    free = {q: 0.0 for q in "VSTGYAN"}
+    pool = {k: {b: 0.0 for b in v_} for k, v_ in POOLS.items()}
+    live, endt, order = {}, [0.0] * n, []
+    ready = [i for i in range(n) if left[i] == 0]
+    while ready:
+        best = None
+        cands = []
+        for i in ready:
+            o = ops[i]
+            est0 = max([endt[d] + (LAT if any(k != "rw" for k, _ in kk) or ops[d]["q"] != o["qs"][0] else 0.0) for d, kk in dep[i].items()] or [0.0])
+            okay = True
+            for b, lo, hi in o["w"]:
+                if isinstance(b, tuple) and tiles[b[1]]["buf"] is None:
+                    tl = tiles[b[1]]
+                    fr = pool[tl["pool"]]
+                    if not fr or (tl["pool"] == "B" and len(fr) < 2 and not live.get(tl["chain"], 0)):
+                        okay = False
+                    else:
+                        est0 = max(est0, min(fr.values()) + LAT)
+            if not okay:
+                continue
+            for q in o["qs"]:
+                cands.append((max(est0, free[q] if q != "N" else 0.0), -rank[i], i, q))
+        assert cands, "no operation can go on"
+        t0 = min(c[0] for c in cands)
+        qsel = [c for c in cands if c[0] <= t0 + 0.03]
+        c = min(qsel, key=lambda c: (c[1], c[0]))
+        st, _, i, q = c
+        o = ops[i]
+        o["q"] = q
+        for b, lo, hi in o["w"]:
+            if isinstance(b, tuple) and tiles[b[1]]["buf"] is None:
+                tl = tiles[b[1]]
+                fr = pool[tl["pool"]]
+                bb = min(fr, key=lambda x: fr[x])
+                del fr[bb]
+                tl["buf"] = bb
+                live[tl["chain"]] = live.get(tl["chain"], 0) + 1
+        e = st + o["dur"]
+        endt[i] = e
+        o["t0"], o["t1"] = st, e
+        free[q] = st + 0.1 if q in "YA" else e
+        if q == "A":
+            free["S"] = max(free["S"], 0.1)
+        for b, lo, hi in o["r"] + o["w"]:
+            if isinstance(b, tuple):
+                tl = tiles[b[1]]
+                tl["users"] -= 1
+                tl["end"] = max(tl.get("end", 0.0), e)
+                if tl["users"] == 0:
+                    pool[tl["pool"]][tl["buf"]] = tl["end"]
+                    live[tl["chain"]] -= 1
+        order.append(i)
+        ready.remove(i)
+        for j in succ[i]:
+            left[j] -= 1
+            if left[j] == 0:
+                ready.append(j)
+    assert len(order) == n
+    seq = [ops[i] for i in order]
+    return seq, tiles, max(endt)
+
+
+PLAN = {}
+
+
+def plan():
+    if not PLAN:
+        seq, tiles, end = schedule()
+        key = lambda b: tiles[b[1]]["buf"] if isinstance(b, tuple) else b
+        PLAN["seq"], PLAN["tiles"], PLAN["end"] = seq, tiles, end
+        PLAN["dep"] = deps_of(seq, key, is_tile)
+    return PLAN
+
+
+def rank_program(g, core, T, topo):
+    rank = T.rank_of(core)
+    if rank is None:
+        return
+    pl = plan()
+    tiles = pl["tiles"]
+    dst = T.cores[(rank + ST) % len(T.cores)]
+    rid, pid, _ = topo.addr(dst)
+    emask = topo.mask(core, dst)
+    ne = len(topo.engines(core, dst))
+    ne_in = len(topo.engines(T.cores[(rank - ST) % len(T.cores)], core))
+    eng = {"V": g.vector, "S": g.scalar, "T": g.tensor, "G": g, "Y": g.sync, "A": g.scalar}
+    host = {"V": "V", "S": "S", "T": "T", "G": "G", "Y": "Y", "A": "S"}
+    ins = {"x": T.x, "r0": T.r0, "c0": T.c0, "yc": T.yc, "yr": T.yr}
+    cur = ["V"]
+
+    def B(name):
+        if name == "Q":
+            return cur[0]
+        if name == "IN":
+            return ins
+        if isinstance(name, tuple):
+            return T[tiles[name[1]]["buf"]]
+        return T[name]
+
+    cnt = {"V": 0, "S": 0, "T": 0, "G": 0}
+    known = {q: {} for q in "VSTGY"}
+    done = {}
+    pend = {}
+
+    def inc(x, q):
+        cnt[q] += 1
+        x.then_inc(T.sem["q" + q], 1)
+
+    for o, dep in zip(pl["seq"], pl["dep"]):
+        q = o["q"]
+        if q == "N":
+            done[o["id"]] = (o["sem"], ne_in, {})
+            pend[o["sem"]] = ne_in
+            continue
+        h = host[q]
+        need = {}
+        for d, kinds in dep.items():
+            sem, c, imp = done[d]
+            if sem == "q" + h:
+                if h == "T" and all(cr for _, cr in kinds):
+                    continue
+                if all(k[0] == "rw" for k in kinds):
+                    continue
+            need[sem] = max(need.get(sem, (0, None))[0], c), imp
+        kn = known[h]
+        for d in sorted(dep, key=lambda d: -done[d][1] if done[d][0] in need else 0):
+            sem, c, imp = done[d]
+            if sem not in need or need[sem][0] != c or kn.get(sem, 0) >= c:
+                continue
+            eng[q].wait_ge(T.sem[sem], c)
+            kn[sem] = c
+            for s2, c2 in imp.items():
+                if kn.get(s2, 0) < c2:
+                    kn[s2] = c2
+        cur[0] = q
+        if isinstance(o["fn"], tuple):
+            _, t, c, j0, j1 = o["fn"]
+            g.remote_dma(T["rf%d" % (t + 1)][:, j0:j1], T["rn%d" % t][:, j0:j1], T.sem[o["sem2"]], T.sem[o["sem"]], pid, rid, emask)
+            done[o["id"]] = (o["sem"], ne, {})
+            pend[o["sem"]] = ne
+        elif o["sem"]:
+            o["fn"](eng[q], B, lambda x: x.then_inc(T.sem[o["sem"]], 16))
+            done[o["id"]] = (o["sem"], 16, dict(kn))
+            pend[o["sem"]] = 16
+        else:
+            o["fn"](eng[q], B, lambda x: inc(x, h))
+            imp = dict(kn)
+            imp["q" + h] = cnt[h]
+            done[o["id"]] = ("q" + h, cnt[h], imp)
+    for q in "VSTG":
+        g.wait_ge(T.sem["q" + q], cnt[q])
+    for sname in pend:
+        if known["G"].get(sname, 0) < pend[sname]:
+            g.wait_ge(T.sem[sname], pend[sname])

@@ -1,85 +1,65 @@
-import math
-from concourse.mybir import AluOpType as A, AxisListType, ActivationFunctionType as F
+from concourse.mybir import AluOpType as A, ActivationFunctionType as F
 
 W, H, P, RO, ST = 3072, 1024, 512, 3, 2
 SH = 1536
 CH = 256
 NC = P // CH
 NL = CH // 16
-RT = 1024 // CH
-KG = 64
+KG = 32
 NAD = 4
+W0 = 128
+RT = 1024 // W0
+KW = CH + 16
 
-SCRATCH = {
-    "xs": ("sbuf", [128, W], "bfloat16"), "r0i": ("sbuf", [128, P], "int32"), "c0i": ("sbuf", [128, H], "int32"),
-    "cache": ("sbuf", [128, H + P], "float32"),
-    "va": ("sbuf", [128, 16 * P], "bfloat16"), "vd": ("sbuf", [128, 16 * P], "bfloat16"),
-    "eqw": ("sbuf", [128, 32 * P], "bfloat16"), "eqp": ("sbuf", [128, 2 * 1024 * NC], "bfloat16"),
-    "rf0": ("sbuf", [128, P], "float16"), "rf1": ("sbuf", [128, P], "float16"), "rf2": ("sbuf", [128, P], "float16"),
-    "rn0": ("sbuf", [128, P], "float16"), "rn1": ("sbuf", [128, P], "float16"),
-    "r2": ("sbuf", [128, P], "float16"), "rp": ("sbuf", [128, P], "float16"),
-    "ru": ("sbuf", [128, P], "uint16"), "rpu": ("sbuf", [128, P], "uint16"),
-    "sb": ("sbuf", [128, P], "bfloat16"), "ind": ("sbuf", [128, P], "bfloat16"), "indr": ("sbuf", [128, P], "float16"),
-    "t1": ("sbuf", [128, P], "float32"), "t2": ("sbuf", [128, P], "float32"),
-    "sf": ("sbuf", [128, P], "bfloat16"), "fr": ("sbuf", [128, P], "float16"), "ee": ("sbuf", [128, P], "bfloat16"),
-    "sm": ("sbuf", [128, P], "bfloat16"), "t3": ("sbuf", [128, P], "float32"),
-    "sb2": ("sbuf", [128, P], "bfloat16"), "ind2": ("sbuf", [128, P], "bfloat16"), "indr2": ("sbuf", [128, P], "float16"),
-    "t4": ("sbuf", [128, P], "float32"), "st": ("sbuf", [128, P], "float32"),
-    "sn": ("sbuf", [128, P], "bfloat16"), "t5": ("sbuf", [128, P], "float32"), "yrs": ("sbuf", [128, P], "float32"),
-    "r15": ("sbuf", [128, 32], "float32"), "rk": ("sbuf", [128, 32], "float32"), "rkk": ("sbuf", [128, 32], "float32"),
-    "pri": ("sbuf", [128, 32], "int32"), "fi": ("sbuf", [128, 32], "int32"), "si": ("sbuf", [128, 32], "int32"),
-    "hm": ("sbuf", [128, 32], "int32"), "nfl": ("sbuf", [128, 32], "float32"), "djn": ("sbuf", [128, 32], "float32"),
-    "hf": ("sbuf", [128, 32], "float32"), "hu": ("sbuf", [128, 32], "uint16"), "hh": ("sbuf", [128, 32], "float16"),
-    "hrep": ("sbuf", [128, P], "float16"), "lose": ("sbuf", [128, P], "bfloat16"),
-    "lt": ("sbuf", [128, 32], "float32"), "lo": ("sbuf", [128, 32], "float32"), "wu": ("sbuf", [128, 32], "uint16"),
-    "ksum": ("sbuf", [128, 8], "float32"), "kcol": ("sbuf", [128, 8], "float32"),
-    "ones": ("sbuf", [128, 2048], "bfloat16"), "c1536": ("sbuf", [128, CH], "bfloat16"), "zero": ("sbuf", [128, 8], "bfloat16"),
-    "onesf": ("sbuf", [128, 128], "float32"),
-    "bo": ("sbuf", [128, 128], "bfloat16"), "bo1": ("sbuf", [128, 128], "bfloat16"), "ey": ("sbuf", [128, 128], "bfloat16"),
-    "ney": ("sbuf", [128, 128], "bfloat16"), "ux": ("sbuf", [128, 128], "bfloat16"), "ux8": ("sbuf", [128, 128], "bfloat16"),
-    "wq": ("sbuf", [128, 128], "bfloat16"), "u15": ("sbuf", [128, 128], "bfloat16"), "u15s": ("sbuf", [128, 128], "bfloat16"),
-    "u15n": ("sbuf", [128, 128], "bfloat16"), "tl": ("sbuf", [128, 128], "bfloat16"), "tl2": ("sbuf", [128, 128], "bfloat16"),
-    "au": ("sbuf", [128, 128], "bfloat16"), "au16": ("sbuf", [128, 128], "bfloat16"),
-    "boq": ("sbuf", [128, 128], "bfloat16"), "boqm": ("sbuf", [128, 128], "bfloat16"), "boqp": ("sbuf", [128, 128], "bfloat16"),
-    "hey": ("sbuf", [128, 128], "bfloat16"),
-    "b8a": ("sbuf", [128, 8], "bfloat16"), "b8": ("sbuf", [128, 8], "bfloat16"), "b15": ("sbuf", [128, 8], "bfloat16"),
-    "mst": ("sbuf", [128, 144], "bfloat16"), "mst15": ("sbuf", [128, 144], "bfloat16"), "mst8": ("sbuf", [128, 144], "bfloat16"),
-    "mqa": ("sbuf", [128, 128], "bfloat16"), "mq": ("sbuf", [128, 128], "bfloat16"),
-    "hq": ("sbuf", [128, 2048], "bfloat16"),
-    "pa": ("sbuf", [128, 1024], "bfloat16"), "pb": ("sbuf", [128, 1024], "bfloat16"),
-    "vm": ("sbuf", [128, 240], "bfloat16"), "vt": ("sbuf", [128, 16], "float32"), "ve": ("sbuf", [128, 16], "float32"),
-    "rio": ("sbuf", [128, 16], "float32"), "ki": ("sbuf", [128, 8], "int32"), "kp": ("sbuf", [128, 8], "int32"),
-    "kd": ("sbuf", [128, 8], "int32"), "ks": ("sbuf", [128, 8], "int32"), "kw": ("sbuf", [128, 8], "int32"),
-    "kf": ("sbuf", [128, 8], "float32"), "indb": ("sbuf", [128, 8], "float32"), "mb": ("sbuf", [128, 8], "float32"),
-    "qm": ("sbuf", [128, 128], "bfloat16"), "qp": ("sbuf", [128, 128], "bfloat16"),
-    "dj": ("sbuf", [128, 32], "float32"),
-    "d0": ("psum", [128, 1024], "float32"), "d1": ("psum", [128, 1024], "float32"),
-    "p0": ("psum", [128, 512], "float32"), "p1": ("psum", [128, 512], "float32"),
-    "p2": ("psum", [128, 512], "float32"), "p3": ("psum", [128, 512], "float32"),
-}
+SCRATCH = {}
+
+
+def bufs(dtype, **sizes):
+    for k in sizes:
+        SCRATCH[k] = ("sbuf", [128, sizes[k]], dtype)
+
+
+bufs("bfloat16", xs=W, va=16 * P, vd=16 * P, eqw=32 * P, eqp=2048 * NC, sb=P, ind=P, sf=P, ee=P, sm=P, sb2=P, ind2=P, sn=P, lose=P,
+     ka=NC * KW, kb=NC * KW, smask=CH)
+bufs("int32", r0i=P, c0i=H, pri=32, fi=32, si=32, hm=32, ki=8, kp=8, kd=8, ks=8, kw=8)
+bufs("float32", cache=H + P, t1=P, t2=P, t3=P, t4=P, st=P, t5=P, yrs=P, r15=32, rkk=32, djn=32, hf=32, lt=32, lo=32, kacc=8, kcol=8,
+     onesf=128, vt=16, ve=16, rio=16, kf=8, mb=8, dj=32)
+bufs("float16", rf0=P, rf1=P, rf2=P, rn0=P, rn1=P, r2=P, rp=P, indr=P, fr=P, indr2=P, hh=32, hrep=P)
+bufs("uint16", ru=P, rpu=P, hu=32, wu=32)
+bufs("bfloat16", ones=2048, c1536=CH, zero=8, bo=128, bo1=128, ey=128, ney=128, ux=128, u15=128, u15s=128, u15n=128, tl=128, tl2=128,
+     au=128, au16=128, boq=128, boqm=128, boqp=128, hey=128, b8a=8, b8=8, b15=8, mst=144, mstn=144, mst15=144, mst8=144, mqa=128, mq=128,
+     hq=2048, pa=1024, pb=1024, vm=240, qm=128, qp=128)
 for _i in range(NAD):
     SCRATCH["ad%d" % _i] = ("sbuf", [128, 1024], "bfloat16")
-LOADS = ["lr", "lx", "lc"]
-SEMAPHORES = (["qV", "qS", "qT", "qG"] + LOADS + ["oc"] + ["oy%d" % c for c in range(NC)]
+for _i in range(2):
+    SCRATCH["d%d" % _i] = ("psum", [128, 1024], "float32")
+for _i in range(4):
+    SCRATCH["p%d" % _i] = ("psum", [128, 512], "float32")
+SEMAPHORES = (["qV", "qS", "qT", "qG", "lr", "lx", "lc", "oc"] + ["oy%d" % c for c in range(NC)]
               + ["ar%d_%d" % (t, c) for t in range(1, RO) for c in range(NC)]
               + ["ls%d_%d" % (t, c) for t in range(1, RO) for c in range(NC)])
 
-CYC, TCYC = 0.00083, 0.00042
+CYC, TCYC, LAT = 0.00083, 0.00042, 0.12
 GF, SCF = 1.56, 3.8
-LAT = 0.12
-POOLS = {"D": ["d0", "d1"], "B": ["p0", "p1", "p2", "p3"]}
+POOLS = {"AD": ["ad%d" % i for i in range(NAD)], "D": ["d0", "d1"], "B": ["p0", "p1", "p2", "p3"]}
+BIAS = {'B00': 19.2, 'P00': 65.9, 'D00': 1.6, 'N00': 36.2, 'E00': 19.2, 'S00': 31.8, 'A00': 3.7, 'H00': 18.5, 'B01': -42.6, 'P01': 11.0,
+        'D01': 18.9, 'N01': 11.2, 'E01': 2.5, 'S01': -15.0, 'A01': -5.5, 'H01': -15.8, 'W00': -20.7, 'B10': 19.0, 'P10': 37.7, 'D10': 8.5,
+        'N10': 13.8, 'E10': -1.6, 'S10': 40.8, 'A10': 0.6, 'H10': 30.5, 'B11': -19.2, 'P11': 26.7, 'D11': 7.0, 'N11': 24.6, 'E11': 6.7,
+        'S11': 56.7, 'A11': 8.6, 'H11': -69.5, 'W10': -0.9, 'B20': -14.7, 'P20': 43.9, 'D20': 2.5, 'N20': 13.2, 'E20': 29.0, 'S20': 5.9,
+        'A20': 1.3, 'H20': 5.4, 'B21': -0.6, 'P21': 1.2, 'D21': 0.6, 'N21': -12.4, 'E21': -14.3, 'S21': -8.9, 'A21': -47.2, 'H21': -0.4,
+        'W20': -2.2, 'C': 2.7}
+QG = {'A01': 'V', 'D11': 'V'}
 
 
 def build_ops():
-    ops, tiles = [], []
+    ops, tiles, cls = [], [], ["C"]
 
     def tile(pool, chain):
         tiles.append({"pool": pool, "chain": chain, "users": 0, "buf": None})
         return ("tile", len(tiles) - 1)
 
-    def op(qs, fn, reads, writes, dur, name="", sem=None, pos=0):
-        ops.append({"qs": qs, "fn": fn, "r": reads, "w": writes, "dur": dur, "name": name, "sem": sem, "id": len(ops)})
-        return len(ops) - 1
+    def op(qs, fn, reads, writes, dur, name="", sem=None):
+        ops.append({"qs": qs, "fn": fn, "r": reads, "w": writes, "dur": dur, "name": name, "sem": sem, "id": len(ops), "cls": cls[0]})
 
     def R(buf, lo=0, hi=None):
         if isinstance(buf, tuple):
@@ -87,20 +67,37 @@ def build_ops():
         return (buf, lo, SCRATCH[buf][1][1] if hi is None else hi)
 
     def v(fn, reads, writes, cyc, name=""):
-        return op("V", fn, reads, writes, 0.055 + CYC * cyc, name)
+        op("V", fn, reads, writes, 0.055 + CYC * cyc, name)
 
     def s(fn, reads, writes, cyc, name=""):
-        return op("S", fn, reads, writes, 0.065 + CYC * cyc, name)
+        op("S", fn, reads, writes, 0.065 + CYC * cyc, name)
 
     def gp(fn, reads, writes, n, name=""):
-        return op("G", fn, reads, writes, 0.17 + 2 * CYC * n, name)
+        op("G", fn, reads, writes, 0.17 + 2 * CYC * n, name)
 
-    def mm(mats, reads, writes, name=""):
-        cols = mats[0]
-        return op("T", mats[1], reads, writes, cols * TCYC + 0.03, name)
+    def mm(cols, fn, reads, writes, name=""):
+        op("T", fn, reads, writes, cols * TCYC + 0.03, name)
 
-    def sel(out, in_, pat, cmp, fill, base, cm, n):
-        return gp(lambda e, B, inc: inc(e.affine_select(out=out(B), in_=in_(B), pattern=pat, compare_op=cmp, fill=fill, base=base, channel_multiplier=cm)), None, None, n)
+    def ts(dst, src, s1, o1, s2=None, o2=None, lo=0, hi=1, cyc=64, slo=None, name="ts", extra=()):
+        a, b = (lo, hi) if slo is None else (slo, slo + hi - lo)
+        val = lambda B, x: B(x[0])[:, x[1]:x[1] + 1] if isinstance(x, tuple) else x
+
+        def fn(e, B, inc):
+            if o2 is None:
+                inc(e.tensor_scalar(out=B(dst)[:, lo:hi], in0=B(src)[:, a:b], scalar1=val(B, s1), scalar2=None, op0=o1))
+            else:
+                inc(e.tensor_scalar(out=B(dst)[:, lo:hi], in0=B(src)[:, a:b], scalar1=val(B, s1), scalar2=val(B, s2), op0=o1, op1=o2))
+        cols = [R(x[0], x[1], x[1] + 1) for x in (s1, s2) if isinstance(x, tuple)]
+        v(fn, [R(src, a, b)] + cols, [R(dst, lo, hi)], cyc, name)
+
+    def tt(dst, in0, in1, o, lo, hi, cyc=None, slo=None, name="tt"):
+        a, b = (lo, hi) if slo is None else (slo, slo + hi - lo)
+        v(lambda e, B, inc: inc(e.tensor_tensor(out=B(dst)[:, lo:hi], in0=B(in0)[:, a:b], in1=B(in1)[:, lo:hi], op=o)),
+          [R(in0, a, b), R(in1, lo, hi)], [R(dst, lo, hi)], (hi - lo) if cyc is None else cyc, name)
+
+    def cp(dst, src, lo, hi, cyc, slo=None, name="cp"):
+        a, b = (lo, hi) if slo is None else (slo, slo + hi - lo)
+        v(lambda e, B, inc: inc(e.tensor_copy(out=B(dst)[:, lo:hi], in_=B(src)[:, a:b])), [R(src, a, b)], [R(dst, lo, hi)], cyc, name)
 
     op("A", lambda e, B, inc: inc(e.dma_start(B("r0i")[:, :], B("IN")["r0"][:, :])), [], [R("r0i")], 2.5, "load r0", sem="lr")
     op("Y", lambda e, B, inc: inc(e.dma_start(B("xs")[:, :], B("IN")["x"][:, :])), [], [R("xs")], 5.0, "load x", sem="lx")
@@ -109,17 +106,14 @@ def build_ops():
     def fill(buf, val, n, lo=0):
         v(lambda e, B, inc: inc(e.memset(B(buf)[:, lo:lo + n], val)), [], [R(buf, lo, lo + n)], n / 2)
 
-    def gsel(dst, src, pat, cmp, fillv, base, cm, n):
-        gp(lambda e, B, inc: inc(e.affine_select(out=B(dst)[:, 0:n], in_=B(src)[:, 0:n], pattern=pat, compare_op=cmp, fill=fillv, base=base, channel_multiplier=cm)),
-           [R(src, 0, n)], [R(dst, 0, n)], n, "sel " + dst)
+    def gsel(dst, src, pat, cmp, fillv, base, cm, n, view=None):
+        w = slice(0, n) if view is None else view
+        gp(lambda e, B, inc: inc(e.affine_select(out=B(dst)[:, w], in_=B(src)[:, w], pattern=pat, compare_op=cmp, fill=fillv, base=base, channel_multiplier=cm)),
+           [R(src)], [R(dst)], n, "sel " + dst)
 
     def scale(dst, src, k):
         n = SCRATCH[src][1][1]
-        v(lambda e, B, inc: inc(e.tensor_scalar(out=B(dst)[:, 0:n], in0=B(src)[:, 0:n], scalar1=float(k), scalar2=None, op0=A.mult)),
-          [R(src)], [R(dst)], n / 2)
-
-    def addm(dst, a, b):
-        v(lambda e, B, inc: inc(e.tensor_tensor(out=B(dst)[:, 0:128], in0=B(a)[:, 0:128], in1=B(b)[:, 0:128], op=A.add)), [R(a), R(b)], [R(dst)], 256)
+        ts(dst, src, float(k), A.mult, hi=n, cyc=n / 2)
 
     fill("ones", 1.0, 2048)
     gsel("ey", "ones", [[-1, 128]], A.is_equal, 0.0, 0, 1, 128)
@@ -131,33 +125,33 @@ def build_ops():
     fill("mst15", 0.0, 144)
     for d_, s_ in (("mst", "b8"), ("mst15", "b15")):
         v(lambda e, B, inc, d_=d_, s_=s_: inc(e.tensor_copy(out=B(d_)[:, 15:143:16], in_=B(s_)[:, 0:8])), [R(s_)], [R(d_)], 64)
+    scale("mstn", "mst", -1)
     gsel("bo1", "ones", [[-16, 8], [0, 16]], A.is_ge, 0.0, 0, 1, 128)
     gsel("bo", "bo1", [[16, 8], [0, 16]], A.is_ge, 0.0, 15, -1, 128)
     gsel("ux", "bo", [[1, 128]], A.is_gt, 0.0, 0, -1, 128)
-    scale("ux8", "ux", -8)
-    gsel("wq", "ux8", [[-1, 128]], A.not_equal, 0.5, 0, 1, 128)
+    fill("smask", 1.0, CH)
+    v(lambda e, B, inc: inc(e.memset(B("smask")[:, 15:CH:16], 0.0)), [], [R("smask")], 64)
+    for c in range(NC):
+        fill("ka", 0.0, 16, c * KW)
+        fill("kb", 0.0, 16, c * KW)
     gsel("u15", "ux", [[0, 8], [-1, 16]], A.is_gt, 0.0, 15, 0, 128)
     scale("u15s", "u15", -SH)
     scale("u15n", "u15", -1)
     gp(lambda e, B, inc: inc(e.iota(B("ki")[:, 0:1], [[0, 1]], 0, 1)), [], [R("ki")], 8)
     gp(lambda e, B, inc: inc(e.iota(B("rio")[:, 0:16], [[1, 16]], 0, 0, allow_small_or_imprecise_dtypes=True)), [], [R("rio")], 16)
     gp(lambda e, B, inc: inc(e.iota(B("dj")[:, 0:32], [[16, 32]], H, 0, allow_small_or_imprecise_dtypes=True)), [], [R("dj")], 32)
-    ts = lambda dst, src, s1, o1, s2=None, o2=None, n=1: v(
-        (lambda e, B, inc: inc(e.tensor_scalar(out=B(dst)[:, 0:n], in0=B(src)[:, 0:n], scalar1=s1, scalar2=None, op0=o1))) if o2 is None else
-        (lambda e, B, inc: inc(e.tensor_scalar(out=B(dst)[:, 0:n], in0=B(src)[:, 0:n], scalar1=s1, scalar2=s2, op0=o1, op1=o2))), [R(src)], [R(dst)], 64)
     ts("kp", "ki", 15, A.bitwise_and)
-    ts("indb", "kp", -8.0, A.mult, 0.5, A.add)
     ts("mb", "kp", 16.0, A.mult, -17.0, A.add)
     ts("kd", "ki", 4, A.arith_shift_right)
-    v(lambda e, B, inc: inc(e.tensor_tensor(out=B("ks")[:, 0:1], in0=B("kp")[:, 0:1], in1=B("kd")[:, 0:1], op=A.add)), [R("kp"), R("kd")], [R("ks")], 64)
+    tt("ks", "kp", "kd", A.add, 0, 1, 64)
     ts("kw", "ks", 1.0, A.add)
     v(lambda e, B, inc: inc(e.tensor_scalar(out=B("ks")[:, 2:3], in0=B("kw")[:, 0:1], scalar1=15, scalar2=None, op0=A.bitwise_and)), [R("kw")], [R("ks")], 64)
-    v(lambda e, B, inc: inc(e.tensor_tensor(out=B("kf")[:, 0:1], in0=B("kp")[:, 0:1], in1=B("ks")[:, 2:3], op=A.min)), [R("kp"), R("ks")], [R("kf")], 64)
-    v(lambda e, B, inc: inc(e.tensor_copy(out=B("kf")[:, 1:2], in_=B("kp")[:, 0:1])), [R("kp")], [R("kf", 1, 2)], 64)
-    v(lambda e, B, inc: inc(e.tensor_scalar(out=B("dj")[:, 0:32], in0=B("dj")[:, 0:32], scalar1=B("kf")[:, 1:2], scalar2=None, op0=A.add)), [R("dj"), R("kf")], [R("dj")], 64)
+    v(lambda e, B, inc: inc(e.tensor_tensor(out=B("kf")[:, 0:1], in0=B("kp")[:, 0:1], in1=B("ks")[:, 2:3], op=A.min)), [R("kp"), R("ks")], [R("kf", 0, 1)], 64)
+    cp("kf", "kp", 1, 2, 64, slo=0)
+    ts("dj", "dj", ("kf", 1), A.add, hi=32)
     fill("vm", 0.0, 240)
-    v(lambda e, B, inc: inc(e.tensor_scalar(out=B("vt")[:, 0:16], in0=B("rio")[:, 0:16], scalar1=B("kf")[:, 0:1], scalar2=-100.0, op0=A.is_gt, op1=A.mult)), [R("rio"), R("kf")], [R("vt")], 64)
-    v(lambda e, B, inc: inc(e.tensor_scalar(out=B("ve")[:, 0:16], in0=B("rio")[:, 0:16], scalar1=B("kf")[:, 0:1], scalar2=None, op0=A.is_equal)), [R("rio"), R("kf")], [R("ve")], 64)
+    ts("vt", "rio", ("kf", 0), A.is_gt, -100.0, A.mult, hi=16)
+    ts("ve", "rio", ("kf", 0), A.is_equal, hi=16)
     v(lambda e, B, inc: inc(e.tensor_tensor(out=B("vm")[:, 112:128], in0=B("vt")[:, 0:16], in1=B("ve")[:, 0:16], op=A.add)), [R("vt"), R("ve")], [R("vm")], 64)
     fill("pa", 0.0, 1024)
     gsel("pb", "pa", [[-16, 8], [0, 8], [-1, 16]], A.not_equal, 1.0, 0, 1, 1024)
@@ -167,8 +161,8 @@ def build_ops():
     gsel("pb", "pa", [[16, 8], [0, 128]], A.is_ge, 0.0, 15, -1, 1024)
     scale("boq", "bo", 0.25)
     scale("hey", "ey", 0.5)
-    addm("boqp", "boq", "hey")
-    v(lambda e, B, inc: inc(e.tensor_tensor(out=B("boqm")[:, 0:128], in0=B("boq")[:, 0:128], in1=B("hey")[:, 0:128], op=A.subtract)), [R("boq"), R("hey")], [R("boqm")], 256)
+    tt("boqp", "boq", "hey", A.add, 0, 128, 256)
+    tt("boqm", "boq", "hey", A.subtract, 0, 128, 256)
     gsel("tl", "bo", [[-1, 128]], A.is_ge, 0.0, 0, 1, 128)
     scale("tl2", "tl", 2)
     gsel("au", "bo", [[1, 128]], A.is_ge, 0.0, 0, -1, 128)
@@ -178,91 +172,105 @@ def build_ops():
     gsel("mq", "mqa", [[1, 16], [16, 8]], A.is_ge, 0.0, -1, -1, 128)
     gsel("mst8", "ones", [[-1, 144]], A.is_equal, 0.0, 15, 16, 144)
     fill("qm", 0.0, 128)
-    gp(lambda e, B, inc: inc(e.affine_select(out=B("qm")[:, 1:128:2], in_=B("qm")[:, 1:128:2], pattern=[[-2, 64]], compare_op=A.not_equal, fill=0.5, base=0, channel_multiplier=1)), [R("qm")], [R("qm")], 64)
-    gp(lambda e, B, inc: inc(e.affine_select(out=B("qm")[:, 1:128:2], in_=B("qm")[:, 1:128:2], pattern=[[-2, 64]], compare_op=A.not_equal, fill=-0.5, base=-1, channel_multiplier=1)), [R("qm")], [R("qm")], 64)
+    gsel("qm", "qm", [[-2, 64]], A.not_equal, 0.5, 0, 1, 64, slice(1, 128, 2))
+    gsel("qm", "qm", [[-2, 64]], A.not_equal, -0.5, -1, 1, 64, slice(1, 128, 2))
     v(lambda e, B, inc: inc(e.memset(B("qm")[:, 15:128:16], 0.0)), [], [R("qm")], 64)
-    addm("qp", "qm", "ey")
+    tt("qp", "qm", "ey", A.add, 0, 128, 256)
     fill("c1536", float(SH), CH)
     fill("onesf", 1.0, 128)
     fill("zero", 0.0, 8)
     fill("cache", 0.0, P, H)
-    v(lambda e, B, inc: inc(e.tensor_copy(out=B("cache")[:, 0:H], in_=B("c0i")[:, :])), [R("c0i")], [R("cache", 0, H)], H)
+    cp("cache", "c0i", 0, H, H)
+    for i, val in ((2, -40.5), (3, 40.5), (4, -0.5)):
+        v(lambda e, B, inc, i=i, val=val: inc(e.memset(B("kf")[:, i:i + 1], val)), [], [R("kf", i, i + 1)], 64)
 
-    adn = [0]
+    def E(B, q, m="mst"):
+        return B(m)[:, 15 - q:143 - q]
 
-    def E(B, p, m="mst"):
-        return B(m)[:, 15 - p:143 - p]
-
-    def dist(vb, c, pairs, chain):
+    def dist(vb, c, pairs, chain, flip):
         ds = tile("B", chain)
-        lo, hi = 16 * c * CH, 16 * (c + 1) * CH
-        for i0 in range(0, len(pairs), RT):
-            part = pairs[i0:i0 + RT]
-            d = tile("D", chain + "d")
-            ad = "ad%d" % (adn[0] % NAD)
-            adn[0] += 1
+        for x in range(CH // W0):
+            for i0 in range(0, len(pairs), RT):
+                part = pairs[i0:i0 + RT]
+                lo, hi = 16 * (c * CH + x * W0), 16 * (c * CH + (x + 1) * W0)
+                d = tile("D", chain + "d")
+                ad = tile("AD", chain + "a")
 
-            def diff(e, B, inc, part=part, d=d):
-                for i, (p, p2, row) in enumerate(part):
-                    o = B(d)[:, i * CH:(i + 1) * CH]
-                    inc(e.matmul(o, B("ey")[:, :], B(vb)[:, lo + p:hi:16], True, False))
-                    inc(e.matmul(o, B("ney")[:, :], B(vb)[:, lo + p2:hi:16], False, True))
-            mm((2 * CH * len(part), diff), [R(vb, lo, hi), R("ey"), R("ney")], [R(d)], "diff")
-            w = CH * len(part)
-            s(lambda e, B, inc, d=d, ad=ad, w=w: inc(e.activation(B(ad)[:, 0:w], B(d)[:, 0:w], F.Abs)), [R(d)], [R(ad)], w, "abs")
+                def diff(e, B, inc, part=part, d=d, lo=lo, hi=hi):
+                    for i, (p, p2, row) in enumerate(part):
+                        o = B(d)[:, i * W0:(i + 1) * W0]
+                        inc(e.matmul(o, B("ey")[:, :], B(vb)[:, lo + p:hi:16], True, False))
+                        inc(e.matmul(o, B("ney")[:, :], B(vb)[:, lo + p2:hi:16], False, True))
+                mm(2 * W0 * len(part), diff, [R(vb, lo, hi), R("ey"), R("ney")], [R(d)], "diff")
+                w = W0 * len(part)
+                s(lambda e, B, inc, d=d, ad=ad, w=w: inc(e.activation(B(ad)[:, 0:w], B(d)[:, 0:w], F.Abs)), [R(d)], [R(ad)], w, "abs")
 
-            def summ(e, B, inc, part=part, ad=ad, i0=i0):
-                for i, (p, p2, row) in enumerate(part):
-                    inc(e.matmul(B(ds)[:, 0:CH], E(B, row), B(ad)[:, i * CH:(i + 1) * CH], i0 + i == 0, i0 + i == len(pairs) - 1))
-            mm((CH * len(part), summ), [R(ad), R("mst")], [R(ds)], "sum")
+                def summ(e, B, inc, part=part, ad=ad, i0=i0, x=x):
+                    for i, (p, p2, row) in enumerate(part):
+                        inc(e.matmul(B(ds)[:, x * W0:(x + 1) * W0], E(B, row), B(ad)[:, i * W0:(i + 1) * W0], i0 + i == 0, i0 + i == len(pairs) - 1))
+
+                def sumf(e, B, inc, part=part, ad=ad, x=x):
+                    b0 = x * W0
+                    for i, (p, p2, row) in enumerate(part):
+                        inc(e.matmul(B(ds)[:, b0 + row:b0 + 128:16], B(ad)[:, i * W0:i * W0 + 128], B("b8")[:, 0:8], True, True))
+                    if part[-1] == pairs[-1]:
+                        inc(e.matmul(B(ds)[:, b0 + 15:b0 + 128:16], B(ad)[:, 0:128], B("zero")[:, 0:8], True, True))
+                if flip:
+                    mm(W0 // 2 * len(part), sumf, [R(ad), R("b8"), R("zero")], [R(ds)], "sum")
+                else:
+                    mm(W0 * len(part), summ, [R(ad), R("mst")], [R(ds)], "sum")
         return ds
 
     def gather(vb, off, c):
         for j in range(c * CH, (c + 1) * CH, KG):
-            def fn(e, B, inc, j=j, q=None):
+            def fn(e, B, inc, j=j):
                 o, w = B(vb)[:, 16 * j:16 * (j + KG)], B("xs")[:, 0:W].indirect(B(off)[:, j:j + KG])
                 if B("Q") == "V":
                     inc(e.tensor_copy(out=o, in_=w))
                 else:
                     inc(e.activation(o, w, F.Copy))
-            op("VS", fn, [R("xs"), R(off, j, j + KG)], [R(vb, 16 * j, 16 * (j + KG))], 0.06 + GF * CYC * 16 * KG, "gather")
+            op(QG.get(cls[0], "VS"), fn, [R("xs"), R(off, j, j + KG)], [R(vb, 16 * j, 16 * (j + KG))], 0.06 + GF * CYC * 16 * KG, "gather")
 
-    def first_fail(ds, c, sbuf, ibuf, chain):
-        j0, j1 = c * CH, (c + 1) * CH
+    def first_fail(ds, c, sbuf, kbuf, ibuf, chain, kacc=None):
+        j0, j1, i0 = c * CH, (c + 1) * CH, 16 + c * KW
         s(lambda e, B, inc: inc(e.activation(B(sbuf)[:, j0:j1], B(ds)[:, 0:CH], F.Sign, bias=B("kf")[:, 2:3])), [R(ds), R("kf")], [R(sbuf, j0, j1)], CH, "bad")
+        v(lambda e, B, inc: inc(e.tensor_tensor_scan(B(kbuf)[:, i0:i0 + CH], B("smask")[:, 0:CH], B(sbuf)[:, j0:j1], 0.0, A.mult, A.max)),
+          [R("smask"), R(sbuf, j0, j1)], [R(kbuf, i0, i0 + CH)], CH / 2, "scan")
         qt = tile("B", chain)
-        mm((CH, lambda e, B, inc: inc(e.matmul(B(qt)[:, 0:CH], B("wq")[:, :], B(sbuf)[:, j0:j1], True, True))), [R("wq"), R(sbuf, j0, j1)], [R(qt)], "q")
 
-        def fn(e, B, inc):
-            if B("Q") == "S":
-                inc(e.activation(B(ibuf)[:, j0:j1], B(qt)[:, 0:CH], F.Relu, bias=B("indb")[:, 0:1]))
-            else:
-                inc(e.tensor_scalar(out=B(ibuf)[:, j0:j1], in0=B(qt)[:, 0:CH], scalar1=B("indb")[:, 0:1], scalar2=0.0, op0=A.add, op1=A.max))
-        op("SV", fn, [R(qt), R("indb")], [R(ibuf, j0, j1)], 0.06 + CYC * CH, "ind")
-
-    for i, val in ((2, -40.5), (3, 40.5), (4, -0.5)):
-        v(lambda e, B, inc, i=i, val=val: inc(e.memset(B("kf")[:, i:i + 1], val)), [], [R("kf", i, i + 1)], 64)
+        def fq(e, B, inc):
+            for x in range(0, CH, 128):
+                inc(e.matmul(B(qt)[:, x:x + 128], B(kbuf)[:, i0 + x:i0 + x + 128], B("ey")[:, :], True, False))
+                inc(e.matmul(B(qt)[:, x:x + 128], B(kbuf)[:, i0 + x - 1:i0 + x + 127], B("ney")[:, :], False, True))
+        mm(2 * CH, fq, [R("ey"), R("ney"), R(kbuf, i0 - 1, i0 + CH)], [R(qt)], "q")
+        if kacc is None:
+            def fn(e, B, inc):
+                if B("Q") == "S":
+                    inc(e.activation(B(ibuf)[:, j0:j1], B(qt)[:, 0:CH], F.Relu))
+                else:
+                    inc(e.tensor_scalar(out=B(ibuf)[:, j0:j1], in0=B(qt)[:, 0:CH], scalar1=0.0, scalar2=None, op0=A.max))
+            op("SV", fn, [R(qt)], [R(ibuf, j0, j1)], 0.06 + CYC * CH, "ind")
+        else:
+            op("S", lambda e, B, inc: inc(e.activation(B(ibuf)[:, j0:j1], B(qt)[:, 0:CH], F.Relu, accum_out=B("kacc")[:, kacc:kacc + 1])),
+               [R(qt)], [R(ibuf, j0, j1), R("kacc", kacc, kacc + 1)], 0.2 + CYC * CH, "ind")
 
     def phase_a(t, c):
-        j0, j1 = c * CH, (c + 1) * CH
-        rf = "rf%d" % t
+        j0, j1, rf, ch = c * CH, (c + 1) * CH, "rf%d" % t, "A%d_%d" % (t, c)
         if t == 0:
-            v(lambda e, B, inc: inc(e.tensor_copy(out=B("ru")[:, j0:j1], in_=B("r0i")[:, j0:j1])), [R("r0i", j0, j1)], [R("ru", j0, j1)], CH, "ru")
-            v(lambda e, B, inc: inc(e.tensor_scalar(out=B(rf)[:, j0:j1], in0=B("r0i")[:, j0:j1], scalar1=float(-SH), scalar2=None, op0=A.add)), [R("r0i", j0, j1)], [R(rf, j0, j1)], CH, "rf")
+            cp("ru", "r0i", j0, j1, CH)
+            ts(rf, "r0i", float(-SH), A.add, lo=j0, hi=j1, cyc=CH)
         else:
-            v(lambda e, B, inc: inc(e.tensor_scalar(out=B("ru")[:, j0:j1], in0=B(rf)[:, j0:j1], scalar1=float(SH), scalar2=None, op0=A.add)), [R(rf, j0, j1)], [R("ru", j0, j1)], CH / 2, "ru")
+            ts("ru", rf, float(SH), A.add, lo=j0, hi=j1, cyc=CH / 2)
         gather("va", "ru", c)
-        ch = "A%d_%d" % (t, c)
         l15 = tile("B", ch + "r")
 
         def f15(e, B, inc):
             for q in range(16):
                 inc(e.matmul(B(l15)[:, 0:NL], E(B, q, "mst15"), B(rf)[:, j0 + q:j1:16], q == 0, q == 15))
-        mm((16 * 64, f15), [R("mst15"), R(rf, j0, j1)], [R(l15)], "r15")
-        v(lambda e, B, inc: inc(e.tensor_scalar(out=B("r15")[:, c * NL:(c + 1) * NL], in0=B(l15)[:, 0:NL], scalar1=float(SH), scalar2=None, op0=A.add)),
-          [R(l15)], [R("r15", c * NL, (c + 1) * NL)], 64, "r15")
-        ds = dist("va", c, [(p, p + 1, p) for p in range(15)], ch)
-        first_fail(ds, c, "sb", "ind", ch)
+        mm(16 * 64, f15, [R("mst15"), R(rf, j0, j1)], [R(l15)], "r15")
+        ts("r15", l15, float(SH), A.add, lo=c * NL, hi=(c + 1) * NL, slo=0, name="r15")
+        ds = dist("va", c, [(p, p + 1, p) for p in range(15)], ch, True)
+        first_fail(ds, c, "sb", "ka", "ind", ch, t * NC + c if t < RO - 1 else None)
 
     def phase_b(t, c):
         j0, j1, k0, k1 = c * CH, (c + 1) * CH, c * NL, (c + 1) * NL
@@ -273,100 +281,102 @@ def build_ops():
             inc(e.matmul(B(wm)[:, 0:CH], B("ey")[:, :], B(rf)[:, j0:j1], True, False))
             inc(e.matmul(B(wm)[:, 0:CH], B("u15s")[:, :], B("ind")[:, j0:j1], False, True))
             inc(e.matmul(B(wm)[:, CH:2 * CH], B("u15")[:, :], B("ind")[:, j0:j1], True, True))
-        mm((3 * CH, fwm), [R("ey"), R("u15"), R("u15s"), R(rf, j0, j1), R("ind", j0, j1)], [R(wm)], "wm")
-        v(lambda e, B, inc: inc(e.tensor_tensor(out=B("indr")[:, j0:j1], in0=B(wm)[:, 0:CH], in1=B("ind")[:, j0:j1], op=A.mult)), [R(wm), R("ind", j0, j1)], [R("indr", j0, j1)], CH, "indr")
+        mm(3 * CH, fwm, [R("ey"), R("u15"), R("u15s"), R(rf, j0, j1), R("ind", j0, j1)]
+           + ([R("kcol", t, t + 1)] if t else []) + ([R("cache")] if t and c else []), [R(wm)], "wm")
+        tt("indr", wm, "ind", A.mult, j0, j1, slo=0, name="indr")
         ll = tile("B", ch)
 
         def ffl(e, B, inc):
             for q in range(16):
-                inc(e.matmul(B(ll)[:, NL:2 * NL], E(B, q), B("ind")[:, j0 + q:j1:16], q == 0, q == 15))
-        mm((16 * 64, ffl), [R("mst"), R("ind", j0, j1)], [R(ll)], "fail list")
+                inc(e.matmul(B(ll)[:, NL:2 * NL], E(B, q, "mstn"), B("ind")[:, j0 + q:j1:16], q == 0, False))
+            inc(e.matmul(B(ll)[:, NL:2 * NL], B("ey")[:, :], B("ones")[:, 0:NL], False, True))
+        mm(17 * 64, ffl, [R("mstn"), R("ey"), R("ones"), R("ind", j0, j1)], [R(ll)], "fail list")
 
         def frk(e, B, inc):
             for q in range(16):
-                inc(e.matmul(B(ll)[:, 0:NL], E(B, q), B("indr")[:, j0 + q:j1:16], q == 0, q == 15))
-        mm((16 * 64, frk), [R("mst"), R("indr", j0, j1)], [R(ll)], "rk list")
-        lst = lambda b: B_(b)
-        v(lambda e, B, inc: inc(e.tensor_scalar(out=B("rk")[:, k0:k1], in0=B(ll)[:, 0:NL], scalar1=float(SH), scalar2=None, op0=A.add)), [R(ll)], [R("rk", k0, k1)], 64, "l")
-        v(lambda e, B, inc: inc(e.tensor_tensor(out=B("pri")[:, k0:k1], in0=B("rk")[:, k0:k1], in1=B("r15")[:, k0:k1], op=A.mult)), [R("rk", k0, k1), R("r15", k0, k1)], [R("pri", k0, k1)], 64, "l")
-        if t == 0:
-            rkk = "rk"
+                inc(e.matmul(B(ll)[:, 0:NL], E(B, q), B("indr")[:, j0 + q:j1:16], q == 0, False))
+            inc(e.matmul(B(ll)[:, 0:NL], B("ey")[:, :], B("c1536")[:, 0:NL], False, True))
+        mm(17 * 64, frk, [R("mst"), R("ey"), R("c1536"), R("indr", j0, j1)], [R(ll)], "rk list")
+        tt("pri", ll, "r15", A.mult, k0, k1, 64, slo=0, name="l")
+        if t:
+            ts("rkk", ll, ("kcol", t), A.add, lo=k0, hi=k1, slo=0, name="l")
+        tt("djn", ll, "dj", A.mult, k0, k1, 64, slo=NL, name="l")
+        ts("fi", "pri", 6, A.arith_shift_right, lo=k0, hi=k1, name="l")
+        if t:
+            tt("si", "rkk", "fi", A.add, k0, k1, 64, name="l")
         else:
-            rkk = "rkk"
-            v(lambda e, B, inc: inc(e.tensor_scalar(out=B("rkk")[:, k0:k1], in0=B(ll)[:, 0:NL], scalar1=float(SH), scalar2=B("kcol")[:, t:t + 1], op0=A.add, op1=A.add)), [R(ll), R("kcol", t, t + 1)], [R("rkk", k0, k1)], 64, "l")
-        v(lambda e, B, inc: inc(e.tensor_scalar(out=B("nfl")[:, k0:k1], in0=B(ll)[:, NL:2 * NL], scalar1=-1.0, scalar2=1.0, op0=A.mult, op1=A.add)), [R(ll)], [R("nfl", k0, k1)], 64, "l")
-        v(lambda e, B, inc: inc(e.tensor_tensor(out=B("djn")[:, k0:k1], in0=B("nfl")[:, k0:k1], in1=B("dj")[:, k0:k1], op=A.mult)), [R("nfl", k0, k1), R("dj")], [R("djn", k0, k1)], 64, "l")
-        v(lambda e, B, inc: inc(e.tensor_scalar(out=B("fi")[:, k0:k1], in0=B("pri")[:, k0:k1], scalar1=6, scalar2=None, op0=A.arith_shift_right)), [R("pri", k0, k1)], [R("fi", k0, k1)], 64, "l")
-        v(lambda e, B, inc: inc(e.tensor_tensor(out=B("si")[:, k0:k1], in0=B("fi")[:, k0:k1], in1=B(rkk)[:, k0:k1], op=A.add)), [R("fi", k0, k1), R(rkk, k0, k1)], [R("si", k0, k1)], 64, "l")
-        v(lambda e, B, inc: inc(e.tensor_scalar(out=B("hm")[:, k0:k1], in0=B("si")[:, k0:k1], scalar1=H - 1, scalar2=None, op0=A.bitwise_and)), [R("si", k0, k1)], [R("hm", k0, k1)], 64, "l")
-        v(lambda e, B, inc: inc(e.tensor_tensor(out=B("hf")[:, k0:k1], in0=B("hm")[:, k0:k1], in1=B("djn")[:, k0:k1], op=A.max)), [R("hm", k0, k1), R("djn", k0, k1)], [R("hf", k0, k1)], 64, "l")
-        v(lambda e, B, inc: inc(e.tensor_copy(out=B("hu")[:, k0:k1], in_=B("hf")[:, k0:k1])), [R("hf", k0, k1)], [R("hu", k0, k1)], 64, "hu")
+            tt("si", ll, "fi", A.add, k0, k1, 64, slo=0, name="l")
+        ts("hm", "si", H - 1, A.bitwise_and, lo=k0, hi=k1, name="l")
+        tt("hf", "hm", "djn", A.max, k0, k1, 64, name="l")
+        cp("hu", "hf", k0, k1, 64, name="hu")
+        cls[0] = "P%d%d" % (t, c)
         v(lambda e, B, inc: inc(e.tensor_tensor(out=B("t1")[:, j0:j1], in0=B("cache")[:, 0:H + P].indirect(B("hu")[:, k0:k1]), in1=B(rf)[:, j0:j1], op=A.subtract)),
           [R("cache"), R("hu", k0, k1), R(rf, j0, j1)], [R("t1", j0, j1)], GF * CH, "cache gather")
-        v(lambda e, B, inc: inc(e.tensor_tensor(out=B("t2")[:, j0:j1], in0=B(wm)[:, CH:2 * CH], in1=B("t1")[:, j0:j1], op=A.mult)), [R(wm), R("t1", j0, j1)], [R("t2", j0, j1)], CH, "t2")
-        v(lambda e, B, inc: inc(e.tensor_tensor(out=B("r2")[:, j0:j1], in0=B(wm)[:, 0:CH], in1=B("t2")[:, j0:j1], op=A.add)), [R(wm), R("t2", j0, j1)], [R("r2", j0, j1)], CH, "r2")
-        gpt = 1024 // CH
-        b0 = c * 2048
+        tt("t2", wm, "t1", A.mult, j0, j1, slo=CH, name="t2")
+        tt("r2", wm, "t2", A.add, j0, j1, slo=0, name="r2")
+        gpt, b0 = 1024 // CH, c * 2048
         for g0 in range(0, 8, gpt):
             d = tile("D", ch + "p")
 
             def fpr(e, B, inc, d=d, g0=g0):
                 for i in range(gpt):
                     inc(e.matmul(B(d)[:, i * CH:(i + 1) * CH], B("pb")[:, 128 * (g0 + i):128 * (g0 + i + 1)], B("r2")[:, j0:j1], True, True))
-            mm((gpt * CH, fpr), [R("pb"), R("r2", j0, j1)], [R(d)], "pairs")
-            v(lambda e, B, inc, d=d, g0=g0: inc(e.tensor_scalar(out=B("eqp")[:, b0 + g0 * CH:b0 + (g0 + gpt) * CH], in0=B(d)[:, 0:gpt * CH], scalar1=0.0, scalar2=None, op0=A.is_equal)),
-              [R(d)], [R("eqp", b0 + g0 * CH, b0 + (g0 + gpt) * CH)], gpt * CH, "eq")
+            mm(gpt * CH, fpr, [R("pb"), R("r2", j0, j1)], [R(d)], "pairs")
+            ts("eqp", d, 0.0, A.is_equal, lo=b0 + g0 * CH, hi=b0 + (g0 + gpt) * CH, cyc=gpt * CH, slo=0, name="eq")
         vt = tile("B", ch)
 
         def fv(e, B, inc):
             for g in range(8):
                 inc(e.matmul(B(vt)[:, 0:CH], B("vm")[:, 112 - 16 * g:240 - 16 * g], B("eqp")[:, b0 + g * CH:b0 + (g + 1) * CH], g == 0, g == 7))
-        mm((8 * CH, fv), [R("vm"), R("eqp", b0, b0 + 8 * CH)], [R(vt)], "V")
+        mm(8 * CH, fv, [R("vm"), R("eqp", b0, b0 + 8 * CH)], [R(vt)], "V")
         s(lambda e, B, inc: inc(e.activation(B("sf")[:, j0:j1], B(vt)[:, 0:CH], F.Sign, bias=B("kf")[:, 4:5])), [R(vt), R("kf")], [R("sf", j0, j1)], CH, "f")
         rc = tile("B", ch)
-        mm((CH, lambda e, B, inc: inc(e.matmul(B(rc)[:, 0:CH], B("ey")[:, :], B("r2")[:, j0:j1], True, True))), [R("ey"), R("r2", j0, j1)], [R(rc)], "copy r2")
-        v(lambda e, B, inc: inc(e.tensor_tensor(out=B("fr")[:, j0:j1], in0=B(rc)[:, 0:CH], in1=B("sf")[:, j0:j1], op=A.mult)), [R(rc), R("sf", j0, j1)], [R("fr", j0, j1)], CH, "fr")
+        mm(CH, lambda e, B, inc: inc(e.matmul(B(rc)[:, 0:CH], B("ey")[:, :], B("r2")[:, j0:j1], True, True)), [R("ey"), R("r2", j0, j1)], [R(rc)], "copy r2")
+        tt("fr", rc, "sf", A.mult, j0, j1, slo=0, name="fr")
         xm = tile("B", ch)
 
         def fxm(e, B, inc):
             inc(e.matmul(B(xm)[:, 0:CH], B("boqm")[:, :], B("r2")[:, j0:j1], True, False))
             inc(e.matmul(B(xm)[:, 0:CH], B("boq")[:, :], B("fr")[:, j0:j1], False, True))
-        mm((2 * CH, fxm), [R("boqm"), R("boq"), R("r2", j0, j1), R("fr", j0, j1)], [R(xm)], "xm")
-        v(lambda e, B, inc: inc(e.tensor_scalar(out=B("ee")[:, j0:j1], in0=B(xm)[:, 0:CH], scalar1=0.0, scalar2=None, op0=A.is_equal)), [R(xm)], [R("ee", j0, j1)], CH, "E")
+        mm(2 * CH, fxm, [R("boqm"), R("boq"), R("r2", j0, j1), R("fr", j0, j1)], [R(xm)], "xm")
+        ts("ee", xm, 0.0, A.is_equal, lo=j0, hi=j1, cyc=CH, slo=0, name="E")
         v2 = tile("B", ch)
 
         def fv2(e, B, inc):
             inc(e.matmul(B(v2)[:, 0:CH], B("au16")[:, :], B("sf")[:, j0:j1], True, False))
             inc(e.matmul(B(v2)[:, 0:CH], B("tl2")[:, :], B("ee")[:, j0:j1], False, True))
-        mm((2 * CH, fv2), [R("au16"), R("tl2"), R("sf", j0, j1), R("ee", j0, j1)], [R(v2)], "v2")
+        mm(2 * CH, fv2, [R("au16"), R("tl2"), R("sf", j0, j1), R("ee", j0, j1)], [R(v2)], "v2")
         s(lambda e, B, inc: inc(e.activation(B("sm")[:, j0:j1], B(v2)[:, 0:CH], F.Sign, bias=B("mb")[:, 0:1])), [R(v2), R("mb")], [R("sm", j0, j1)], CH, "M")
-        v(lambda e, B, inc: inc(e.tensor_tensor(out=B("t3")[:, j0:j1], in0=B(xm)[:, 0:CH], in1=B("sm")[:, j0:j1], op=A.mult)), [R(xm), R("sm", j0, j1)], [R("t3", j0, j1)], CH, "t3")
+        tt("t3", xm, "sm", A.mult, j0, j1, slo=0, name="t3")
         xp = tile("B", ch)
 
         def fxp(e, B, inc):
             inc(e.matmul(B(xp)[:, 0:CH], B("boqp")[:, :], B("r2")[:, j0:j1], True, False))
             inc(e.matmul(B(xp)[:, 0:CH], B("boq")[:, :], B("fr")[:, j0:j1], False, True))
-        mm((2 * CH, fxp), [R("boqp"), R("boq"), R("r2", j0, j1), R("fr", j0, j1), R("sm", j0, j1)], [R(xp)], "xp")
-        v(lambda e, B, inc: inc(e.tensor_tensor(out=B("rp")[:, j0:j1], in0=B(xp)[:, 0:CH], in1=B("t3")[:, j0:j1], op=A.add)), [R(xp), R("t3", j0, j1)], [R("rp", j0, j1)], CH, "rp")
-        v(lambda e, B, inc: inc(e.tensor_scalar(out=B("rpu")[:, j0:j1], in0=B("rp")[:, j0:j1], scalar1=float(SH), scalar2=None, op0=A.add)), [R("rp", j0, j1)], [R("rpu", j0, j1)], CH / 2, "rpu")
+        mm(2 * CH, fxp, [R("boqp"), R("boq"), R("r2", j0, j1), R("fr", j0, j1), R("sm", j0, j1)], [R(xp)], "xp")
+        tt("rp", xp, "t3", A.add, j0, j1, slo=0, name="rp")
+        ts("rpu", "rp", float(SH), A.add, lo=j0, hi=j1, cyc=CH / 2, name="rpu")
 
     def hrep(t, c):
         j0, j1, k0, k1 = c * CH, (c + 1) * CH, c * NL, (c + 1) * NL
-        v(lambda e, B, inc: inc(e.tensor_copy(out=B("hh")[:, k0:k1], in_=B("hf")[:, k0:k1])), [R("hf", k0, k1)], [R("hh", k0, k1)], 64, "hh")
+        cp("hh", "hf", k0, k1, 64, name="hh")
         hr = tile("B", "H%d_%d" % (t, c))
 
         def fh(e, B, inc):
             for q in range(16):
                 inc(e.matmul(B(hr)[:, q:CH:16], B("hq")[:, 128 * q:128 * (q + 1)], B("hh")[:, k0:k1], True, True))
-        mm((16 * 64, fh), [R("hq"), R("hh", k0, k1)], [R(hr)], "hrep")
-        v(lambda e, B, inc: inc(e.tensor_copy(out=B("hrep")[:, j0:j1], in_=B(hr)[:, 0:CH])), [R(hr)], [R("hrep", j0, j1)], CH, "hrep")
+        mm(16 * 64, fh, [R("hq"), R("hh", k0, k1)], [R(hr)], "hrep")
+        cp("hrep", hr, j0, j1, CH, slo=0, name="hrep")
 
     def winners(t):
         if t < RO - 1:
-            v(lambda e, B, inc: inc(e.tensor_reduce(out=B("ksum")[:, t:t + 1], in_=B("nfl")[:, 0:32], axis=AxisListType.X, op=A.add)), [R("nfl")], [R("ksum", t, t + 1)], 64, "K")
             kt = tile("B", "K%d" % t)
-            mm((256, lambda e, B, inc: inc(e.matmul(B(kt)[:, 0:1], B("onesf")[:, :], B("ksum")[:, t:t + 1], True, True))), [R("onesf"), R("ksum", t, t + 1)], [R(kt)], "K")
-            v(lambda e, B, inc: inc(e.tensor_scalar(out=B("kcol")[:, t + 1:t + 2], in0=B(kt)[:, 0:1], scalar1=-1.0, scalar2=float(8 * P), op0=A.mult, op1=A.add)), [R(kt)], [R("kcol", t + 1, t + 2)], 64, "K")
+
+            def fk(e, B, inc):
+                for c in range(NC):
+                    inc(e.matmul(B(kt)[:, 0:1], B("onesf")[:, :], B("kacc")[:, t * NC + c:t * NC + c + 1], c == 0, c == NC - 1))
+            mm(256 * NC, fk, [R("onesf"), R("kacc", t * NC, t * NC + NC)], [R(kt)], "K")
+            cp("kcol", kt, t + 1, t + 2, 64, slo=0, name="K")
         for k in range(32):
             n = P - 16 * k
             v(lambda e, B, inc, k=k, n=n: inc(e.tensor_scalar(out=B("eqw")[:, P * k:P * k + n], in0=B("hrep")[:, 16 * k:P], scalar1=B("hf")[:, k:k + 1], scalar2=None, op0=A.is_equal)),
@@ -378,47 +388,45 @@ def build_ops():
                     inc(e.matmul(B(z)[0:8, 0:P], B("zero")[:, 0:8], B("eqw")[:, 0:P], True, False))
                 for k in range(k0, min(k0 + 4, 31)):
                     inc(e.matmul(B(z)[0:8, 16 * (k + 1):P], B("b8")[:, 0:8], B("eqw")[:, P * k + 16:P * k + P - 16 * k], False, False))
-            mm((4 * (P - 16 * k0), fz), [R("zero"), R("b8"), R("eqw", P * k0, P * (k0 + 3) + P - 16 * (k0 + 3))], [R(z)], "Z")
+            mm(4 * (P - 16 * k0), fz, [R("zero"), R("b8"), R("eqw", P * k0, P * (k0 + 3) + P - 16 * (k0 + 3))], [R(z)], "Z")
 
         def fzd(e, B, inc):
             for q in range(16):
                 inc(e.matmul(B(z)[0:8, q:P:16], B("mq")[:, 8 * q:8 * q + 8], B("eqw")[:, q:32 * P:P], False, q == 15))
-        mm((16 * 32, fzd), [R("mq"), R("eqw")], [R(z)], "Zd")
+        mm(16 * 32, fzd, [R("mq"), R("eqw")], [R(z)], "Zd")
         s(lambda e, B, inc: inc(e.activation(B("lose")[0:8, 0:P], B(z)[0:8, 0:P], F.Sign)), [R(z)], [R("lose")], P, "lose")
         wl = tile("B", "W%d" % t)
 
         def fl(e, B, inc):
             for q in range(16):
                 inc(e.matmul(B(wl)[:, 0:32], B("mst8")[0:8, 15 - q:143 - q], B("lose")[0:8, q:P:16], q == 0, q == 15))
-        mm((16 * 64, fl), [R("mst8"), R("lose")], [R(wl)], "lose list")
-        v(lambda e, B, inc: inc(e.tensor_tensor(out=B("lt")[:, 0:32], in0=B(wl)[:, 0:32], in1=B("dj")[:, 0:32], op=A.mult)), [R(wl), R("dj")], [R("lt")], 64, "w")
-        v(lambda e, B, inc: inc(e.tensor_tensor(out=B("lo")[:, 0:32], in0=B("lt")[:, 0:32], in1=B("hf")[:, 0:32], op=A.max)), [R("lt"), R("hf")], [R("lo")], 64, "w")
-        v(lambda e, B, inc: inc(e.tensor_copy(out=B("wu")[:, 0:32], in_=B("lo")[:, 0:32])), [R("lo")], [R("wu")], 64, "w")
+        mm(16 * 64, fl, [R("mst8"), R("lose")], [R(wl)], "lose list")
+        tt("lt", wl, "dj", A.mult, 0, 32, 64, name="w")
+        tt("lo", "lt", "hf", A.max, 0, 32, 64, name="w")
+        cp("wu", "lo", 0, 32, 64, name="w")
 
     def phase_d(t, c):
         ch = "D%d_%d" % (t, c)
         gather("vd", "rpu", c)
-        ds = dist("vd", c, [(p, p + 1, p) for p in range(15)], ch)
-        first_fail(ds, c, "sb2", "ind2", ch)
-        return dist("vd", c, [(p, p + 2, p + 1) for p in range(0, 14, 2)], ch + "n")
+        ds = dist("vd", c, [(p, p + 1, p) for p in range(15)], ch, True)
+        first_fail(ds, c, "sb2", "kb", "ind2", ch)
+        cls[0] = "N%d%d" % (t, c)
+        return dist("vd", c, [(p, p + 2, p + 1) for p in range(0, 14, 2)], ch + "n", False)
 
     def phase_e(t, c, dn):
-        j0, j1 = c * CH, (c + 1) * CH
-        ch = "E%d_%d" % (t, c)
+        j0, j1, ch = c * CH, (c + 1) * CH, "E%d_%d" % (t, c)
         s(lambda e, B, inc: inc(e.activation(B("sn")[:, j0:j1], B(dn)[:, 0:CH], F.Sign, scale=-1.0, bias=B("kf")[:, 3:4])), [R(dn), R("kf")], [R("sn", j0, j1)], CH, "near")
         n1 = tile("B", ch + "n")
 
         def f6(e, B, inc):
             inc(e.matmul(B(n1)[:, 0:CH], B("qm")[:, :], B("rp")[:, j0:j1], True, True))
+            inc(e.matmul(B(n1)[:, CH:2 * CH], B("qp")[:, :], B("rp")[:, j0:j1], True, t < RO - 1))
             if t == RO - 1:
-                inc(e.matmul(B(n1)[:, CH:2 * CH], B("qp")[:, :], B("rp")[:, j0:j1], True, False))
                 inc(e.matmul(B(n1)[:, CH:2 * CH], B("ey")[:, :], B("c1536")[:, :], False, True))
-            else:
-                inc(e.matmul(B(n1)[:, CH:2 * CH], B("qp")[:, :], B("rp")[:, j0:j1], True, True))
-        mm((2 * CH, f6), [R("qm"), R("qp"), R("ey"), R("c1536"), R("rp", j0, j1), R("sn", j0, j1)], [R(n1)], "n1")
-        v(lambda e, B, inc: inc(e.tensor_tensor(out=B("t5")[:, j0:j1], in0=B(n1)[:, 0:CH], in1=B("sn")[:, j0:j1], op=A.mult)), [R(n1), R("sn", j0, j1)], [R("t5", j0, j1)], CH, "t5")
+        mm(2 * CH, f6, [R("qm"), R("qp"), R("ey"), R("c1536"), R("rp", j0, j1), R("sn", j0, j1)], [R(n1)], "n1")
+        tt("t5", n1, "sn", A.mult, j0, j1, slo=0, name="t5")
         out = "yrs" if t == RO - 1 else "rn%d" % t
-        v(lambda e, B, inc: inc(e.tensor_tensor(out=B(out)[:, j0:j1], in0=B(n1)[:, CH:2 * CH], in1=B("t5")[:, j0:j1], op=A.add)), [R(n1), R("t5", j0, j1)], [R(out, j0, j1)], CH, "rn")
+        tt(out, n1, "t5", A.add, j0, j1, slo=CH, name="rn")
         if t == RO - 1:
             op("Y", lambda e, B, inc: inc(e.dma_start(B("IN")["yr"][:, j0:j1], B("yrs")[:, j0:j1])), [R("yrs", j0, j1)], [("yr", j0, j1)], 2.5, "store yr", sem="oy%d" % c)
         else:
@@ -426,41 +434,49 @@ def build_ops():
             ops[-1]["sem2"] = "ar%d_%d" % (t + 1, c)
             op("N", ("arrive", t + 1, c), [R(out, j0, j1)], [R("rf%d" % (t + 1), j0, j1)], 3.5, "arrive", sem="ar%d_%d" % (t + 1, c))
             ops[-1]["after"] = len(ops) - 2
+        cls[0] = "S%d%d" % (t, c)
         om = tile("B", ch)
 
         def fom(e, B, inc):
             inc(e.matmul(B(om)[:, 0:CH], B("ey")[:, :], B("ones")[:, 0:CH], True, False))
             inc(e.matmul(B(om)[:, 0:CH], B("u15n")[:, :], B("ind2")[:, j0:j1], False, True))
             inc(e.matmul(B(om)[:, CH:2 * CH], B("ey")[:, :], B("rp")[:, j0:j1], True, True))
-        mm((3 * CH, fom), [R("ey"), R("ones"), R("u15n"), R("ind2", j0, j1), R("rp", j0, j1)], [R(om)], "om")
-        v(lambda e, B, inc: inc(e.tensor_tensor(out=B("indr2")[:, j0:j1], in0=B(om)[:, CH:2 * CH], in1=B("ind2")[:, j0:j1], op=A.mult)), [R(om), R("ind2", j0, j1)], [R("indr2", j0, j1)], CH, "indr2")
-        v(lambda e, B, inc: inc(e.tensor_tensor(out=B("t4")[:, j0:j1], in0=B(om)[:, 0:CH], in1=B("rp")[:, j0:j1], op=A.mult)), [R(om), R("rp", j0, j1)], [R("t4", j0, j1)], CH, "t4")
+        mm(3 * CH, fom, [R("ey"), R("ones"), R("u15n"), R("ind2", j0, j1), R("rp", j0, j1)], [R(om)], "om")
+        tt("indr2", om, "ind2", A.mult, j0, j1, slo=CH, name="indr2")
+        tt("t4", om, "rp", A.mult, j0, j1, slo=0, name="t4")
         sk = tile("B", ch)
 
         def fsk(e, B, inc):
             inc(e.matmul(B(sk)[:, 0:CH], B("ey")[:, :], B("c1536")[:, :], True, False))
             inc(e.matmul(B(sk)[:, 0:CH], B("u15")[:, :], B("indr2")[:, j0:j1], False, True))
-        mm((2 * CH, fsk), [R("ey"), R("c1536"), R("u15"), R("indr2", j0, j1)], [R(sk)], "sk")
-        v(lambda e, B, inc: inc(e.tensor_tensor(out=B("st")[:, j0:j1], in0=B(sk)[:, 0:CH], in1=B("t4")[:, j0:j1], op=A.add)), [R(sk), R("t4", j0, j1)], [R("st", j0, j1)], CH, "st")
+        mm(2 * CH, fsk, [R("ey"), R("c1536"), R("u15"), R("indr2", j0, j1)], [R(sk)], "sk")
+        tt("st", sk, "t4", A.add, j0, j1, slo=0, name="st")
+        k0, k1 = c * NL, (c + 1) * NL
+        v(lambda e, B, inc: inc(e.tensor_copy(out=B("cache")[:, 0:H + P].indirect(B("wu")[:, k0:k1]), in_=B("st")[:, j0:j1])),
+          [R("wu", k0, k1), R("st", j0, j1)], [R("cache")], SCF * CH, "scatter")
 
     for t in range(RO):
         for c in range(NC):
+            cls[0] = "A%d%d" % (t, c)
             phase_a(t, c)
         for c in range(NC):
+            cls[0] = "B%d%d" % (t, c)
             phase_b(t, c)
+            cls[0] = "H%d%d" % (t, c)
             hrep(t, c)
+        cls[0] = "W%d0" % t
         winners(t)
         for c in range(NC):
+            cls[0] = "D%d%d" % (t, c)
             dn = phase_d(t, c)
+            cls[0] = "E%d%d" % (t, c)
             phase_e(t, c, dn)
-        v(lambda e, B, inc: inc(e.tensor_copy(out=B("cache")[:, 0:H + P].indirect(B("wu")[:, 0:32]), in_=B("st")[:, :])), [R("wu"), R("st")], [R("cache")], SCF * P, "scatter")
     op("Y", lambda e, B, inc: inc(e.dma_start(B("IN")["yc"][:, :], B("cache")[:, 0:H])), [R("cache", 0, H)], [("yc", 0, H)], 3.0, "store yc", sem="oc")
     return ops, tiles
 
 
 def deps_of(ops, key, cross):
-    hist = {}
-    out = []
+    hist, out = {}, []
     for o in ops:
         d = {}
         for rw, regs in (("r", o["r"]), ("w", o["w"])):
@@ -484,8 +500,11 @@ def deps_of(ops, key, cross):
     return out
 
 
+PSUM = set(k for k in SCRATCH if SCRATCH[k][0] == "psum")
+
+
 def is_tile(b):
-    return isinstance(b, tuple) or b in ("d0", "d1", "p0", "p1", "p2", "p3")
+    return b in PSUM
 
 
 def schedule():
@@ -495,23 +514,23 @@ def schedule():
         for b, lo, hi in o["r"] + o["w"]:
             if isinstance(b, tuple):
                 tiles[b[1]]["users"] += 1
-    dep = deps_of(ops, lambda b: b, is_tile)
+    dep = deps_of(ops, lambda b: b, lambda b: isinstance(b, tuple) and tiles[b[1]]["pool"] != "AD")
     n = len(ops)
     succ = [[] for _ in range(n)]
-    left = [0] * n
+    left = [len(dep[i]) for i in range(n)]
     for i in range(n):
-        left[i] = len(dep[i])
         for d in dep[i]:
             succ[d].append(i)
     rank = [0.0] * n
     for i in range(n - 1, -1, -1):
         rank[i] = ops[i]["dur"] + max([rank[j] + LAT for j in succ[i]] or [0.0])
+    for i in range(n):
+        rank[i] += BIAS.get(ops[i]["cls"], 0.0)
     free = {q: 0.0 for q in "VSTGYAN"}
     pool = {k: {b: 0.0 for b in v_} for k, v_ in POOLS.items()}
     live, endt, order = {}, [0.0] * n, []
     ready = [i for i in range(n) if left[i] == 0]
     while ready:
-        best = None
         cands = []
         for i in ready:
             o = ops[i]
@@ -525,15 +544,12 @@ def schedule():
                         okay = False
                     else:
                         est0 = max(est0, min(fr.values()) + LAT)
-            if not okay:
-                continue
-            for q in o["qs"]:
-                cands.append((max(est0, free[q] if q != "N" else 0.0), -rank[i], i, q))
+            if okay:
+                for q in o["qs"]:
+                    cands.append((max(est0, free[q] if q != "N" else 0.0), -rank[i], i, q))
         assert cands, "no operation can go on"
         t0 = min(c[0] for c in cands)
-        qsel = [c for c in cands if c[0] <= t0 + 0.03]
-        c = min(qsel, key=lambda c: (c[1], c[0]))
-        st, _, i, q = c
+        st, _, i, q = min([c for c in cands if c[0] <= t0 + 0.03], key=lambda c: (c[1], c[0]))
         o = ops[i]
         o["q"] = q
         for b, lo, hi in o["w"]:
@@ -545,8 +561,7 @@ def schedule():
                 tl["buf"] = bb
                 live[tl["chain"]] = live.get(tl["chain"], 0) + 1
         e = st + o["dur"]
-        endt[i] = e
-        o["t0"], o["t1"] = st, e
+        endt[i], o["t0"], o["t1"] = e, st, e
         free[q] = st + 0.1 if q in "YA" else e
         if q == "A":
             free["S"] = max(free["S"], 0.1)
@@ -565,8 +580,7 @@ def schedule():
             if left[j] == 0:
                 ready.append(j)
     assert len(order) == n
-    seq = [ops[i] for i in order]
-    return seq, tiles, max(endt)
+    return [ops[i] for i in order], tiles, max(endt)
 
 
 PLAN = {}
@@ -577,7 +591,7 @@ def plan():
         seq, tiles, end = schedule()
         key = lambda b: tiles[b[1]]["buf"] if isinstance(b, tuple) else b
         PLAN["seq"], PLAN["tiles"], PLAN["end"] = seq, tiles, end
-        PLAN["dep"] = deps_of(seq, key, is_tile)
+        PLAN["dep"] = deps_of(seq, key, lambda b: is_tile(key(b)))
     return PLAN
 
 
@@ -588,10 +602,9 @@ def rank_program(g, core, T, topo):
     pl = plan()
     tiles = pl["tiles"]
     dst = T.cores[(rank + ST) % len(T.cores)]
+    src = T.cores[(rank - ST) % len(T.cores)]
     rid, pid, _ = topo.addr(dst)
-    emask = topo.mask(core, dst)
-    ne = len(topo.engines(core, dst))
-    ne_in = len(topo.engines(T.cores[(rank - ST) % len(T.cores)], core))
+    emask, ne, ne_in = topo.mask(core, dst), len(topo.engines(core, dst)), len(topo.engines(src, core))
     eng = {"V": g.vector, "S": g.scalar, "T": g.tensor, "G": g, "Y": g.sync, "A": g.scalar}
     host = {"V": "V", "S": "S", "T": "T", "G": "G", "Y": "Y", "A": "S"}
     ins = {"x": T.x, "r0": T.r0, "c0": T.c0, "yc": T.yc, "yr": T.yr}
@@ -602,14 +615,11 @@ def rank_program(g, core, T, topo):
             return cur[0]
         if name == "IN":
             return ins
-        if isinstance(name, tuple):
-            return T[tiles[name[1]]["buf"]]
-        return T[name]
+        return T[tiles[name[1]]["buf"]] if isinstance(name, tuple) else T[name]
 
     cnt = {"V": 0, "S": 0, "T": 0, "G": 0}
     known = {q: {} for q in "VSTGY"}
-    done = {}
-    pend = {}
+    done, pend = {}, {}
 
     def inc(x, q):
         cnt[q] += 1
@@ -622,25 +632,22 @@ def rank_program(g, core, T, topo):
             pend[o["sem"]] = ne_in
             continue
         h = host[q]
-        need = {}
+        kn, need = known[h], {}
         for d, kinds in dep.items():
             sem, c, imp = done[d]
             if sem == "q" + h:
-                if h == "T" and all(cr for _, cr in kinds):
+                if (h == "T" and all(cr for _, cr in kinds)) or all(k == "rw" for k, _ in kinds):
                     continue
-                if all(k[0] == "rw" for k in kinds):
-                    continue
-            need[sem] = max(need.get(sem, (0, None))[0], c), imp
-        kn = known[h]
-        for d in sorted(dep, key=lambda d: -done[d][1] if done[d][0] in need else 0):
-            sem, c, imp = done[d]
-            if sem not in need or need[sem][0] != c or kn.get(sem, 0) >= c:
+            if c > need.get(sem, (0, None))[0]:
+                need[sem] = (c, imp)
+        for sem in sorted(need, key=lambda x: -need[x][0]):
+            c, imp = need[sem]
+            if kn.get(sem, 0) >= c:
                 continue
             eng[q].wait_ge(T.sem[sem], c)
             kn[sem] = c
             for s2, c2 in imp.items():
-                if kn.get(s2, 0) < c2:
-                    kn[s2] = c2
+                kn[s2] = max(kn.get(s2, 0), c2)
         cur[0] = q
         if isinstance(o["fn"], tuple):
             _, t, c, j0, j1 = o["fn"]

from concourse.mybir import AluOpType as A, ActivationFunctionType as F

W, H, P, RO, ST = 3072, 1024, 512, 3, 2
SH = 1536
CH = 256
NC = P // CH
NL = CH // 16
KG = 32
NAD = 4
W0 = 128
RT = 1024 // W0
KW = CH + 16

SCRATCH = {}


def bufs(dtype, **sizes):
    for k in sizes:
        SCRATCH[k] = ("sbuf", [128, sizes[k]], dtype)


bufs("bfloat16", xs=W, va=16 * P, vd=16 * P, eqw=32 * P, eqp=2048 * NC, sb=P, ind=P, sf=P, ee=P, sm=P, sb2=P, ind2=P, sn=P, lose=P,
     ka=NC * KW, kb=NC * KW, smask=CH)
bufs("int32", r0i=P, c0i=H, pri=32, fi=32, si=32, hm=32, ki=8, kp=8, kd=8, ks=8, kw=8)
bufs("float32", cache=H + P, t1=P, t2=P, t3=P, t4=P, st=P, t5=P, yrs=P, r15=32, rkk=32, djn=32, hf=32, lt=32, lo=32, kacc=8, kcol=8,
     onesf=128, vt=16, ve=16, rio=16, kf=8, mb=8, dj=32)
bufs("float16", rf0=P, rf1=P, rf2=P, rn0=P, rn1=P, r2=P, rp=P, indr=P, fr=P, indr2=P, hh=32, hrep=P)
bufs("uint16", ru=P, rpu=P, hu=32, wu=32)
bufs("bfloat16", ones=2048, c1536=CH, zero=8, bo=128, bo1=128, ey=128, ney=128, ux=128, u15=128, u15s=128, u15n=128, tl=128, tl2=128,
     au=128, au16=128, boq=128, boqm=128, boqp=128, hey=128, b8a=8, b8=8, b15=8, mst=144, mstn=144, mst15=144, mst8=144, mqa=128, mq=128,
     hq=2048, pa=1024, pb=1024, vm=240, qm=128, qp=128)
for _i in range(NAD):
    SCRATCH["ad%d" % _i] = ("sbuf", [128, 1024], "bfloat16")
for _i in range(2):
    SCRATCH["d%d" % _i] = ("psum", [128, 1024], "float32")
for _i in range(4):
    SCRATCH["p%d" % _i] = ("psum", [128, 512], "float32")
SEMAPHORES = (["qV", "qS", "qT", "qG", "lr", "lx", "lc", "oc"] + ["oy%d" % c for c in range(NC)]
              + ["ar%d_%d" % (t, c) for t in range(1, RO) for c in range(NC)]
              + ["ls%d_%d" % (t, c) for t in range(1, RO) for c in range(NC)])

CYC, TCYC, LAT = 0.00083, 0.00042, 0.12
GF, SCF = 1.56, 3.8
POOLS = {"AD": ["ad%d" % i for i in range(NAD)], "D": ["d0", "d1"], "B": ["p0", "p1", "p2", "p3"]}
BIAS = {'B00': 19.2, 'P00': 65.9, 'D00': 1.6, 'N00': 36.2, 'E00': 19.2, 'S00': 31.8, 'A00': 3.7, 'H00': 18.5, 'B01': -42.6, 'P01': 11.0,
        'D01': 18.9, 'N01': 11.2, 'E01': 2.5, 'S01': -15.0, 'A01': -5.5, 'H01': -15.8, 'W00': -20.7, 'B10': 19.0, 'P10': 37.7, 'D10': 8.5,
        'N10': 13.8, 'E10': -1.6, 'S10': 40.8, 'A10': 0.6, 'H10': 30.5, 'B11': -19.2, 'P11': 26.7, 'D11': 7.0, 'N11': 24.6, 'E11': 6.7,
        'S11': 56.7, 'A11': 8.6, 'H11': -69.5, 'W10': -0.9, 'B20': -14.7, 'P20': 43.9, 'D20': 2.5, 'N20': 13.2, 'E20': 29.0, 'S20': 5.9,
        'A20': 1.3, 'H20': 5.4, 'B21': -0.6, 'P21': 1.2, 'D21': 0.6, 'N21': -12.4, 'E21': -14.3, 'S21': -8.9, 'A21': -47.2, 'H21': -0.4,
        'W20': -2.2, 'C': 2.7}
QG = {'A01': 'V', 'D11': 'V'}


def build_ops():
    ops, tiles, cls = [], [], ["C"]

    def tile(pool, chain):
        tiles.append({"pool": pool, "chain": chain, "users": 0, "buf": None})
        return ("tile", len(tiles) - 1)

    def op(qs, fn, reads, writes, dur, name="", sem=None):
        ops.append({"qs": qs, "fn": fn, "r": reads, "w": writes, "dur": dur, "name": name, "sem": sem, "id": len(ops), "cls": cls[0]})

    def R(buf, lo=0, hi=None):
        if isinstance(buf, tuple):
            return (buf, 0, 512)
        return (buf, lo, SCRATCH[buf][1][1] if hi is None else hi)

    def v(fn, reads, writes, cyc, name=""):
        op("V", fn, reads, writes, 0.055 + CYC * cyc, name)

    def s(fn, reads, writes, cyc, name=""):
        op("S", fn, reads, writes, 0.065 + CYC * cyc, name)

    def gp(fn, reads, writes, n, name=""):
        op("G", fn, reads, writes, 0.17 + 2 * CYC * n, name)

    def mm(cols, fn, reads, writes, name=""):
        op("T", fn, reads, writes, cols * TCYC + 0.03, name)

    def ts(dst, src, s1, o1, s2=None, o2=None, lo=0, hi=1, cyc=64, slo=None, name="ts", extra=()):
        a, b = (lo, hi) if slo is None else (slo, slo + hi - lo)
        val = lambda B, x: B(x[0])[:, x[1]:x[1] + 1] if isinstance(x, tuple) else x

        def fn(e, B, inc):
            if o2 is None:
                inc(e.tensor_scalar(out=B(dst)[:, lo:hi], in0=B(src)[:, a:b], scalar1=val(B, s1), scalar2=None, op0=o1))
            else:
                inc(e.tensor_scalar(out=B(dst)[:, lo:hi], in0=B(src)[:, a:b], scalar1=val(B, s1), scalar2=val(B, s2), op0=o1, op1=o2))
        cols = [R(x[0], x[1], x[1] + 1) for x in (s1, s2) if isinstance(x, tuple)]
        v(fn, [R(src, a, b)] + cols, [R(dst, lo, hi)], cyc, name)

    def tt(dst, in0, in1, o, lo, hi, cyc=None, slo=None, name="tt"):
        a, b = (lo, hi) if slo is None else (slo, slo + hi - lo)
        v(lambda e, B, inc: inc(e.tensor_tensor(out=B(dst)[:, lo:hi], in0=B(in0)[:, a:b], in1=B(in1)[:, lo:hi], op=o)),
          [R(in0, a, b), R(in1, lo, hi)], [R(dst, lo, hi)], (hi - lo) if cyc is None else cyc, name)

    def cp(dst, src, lo, hi, cyc, slo=None, name="cp"):
        a, b = (lo, hi) if slo is None else (slo, slo + hi - lo)
        v(lambda e, B, inc: inc(e.tensor_copy(out=B(dst)[:, lo:hi], in_=B(src)[:, a:b])), [R(src, a, b)], [R(dst, lo, hi)], cyc, name)

    op("A", lambda e, B, inc: inc(e.dma_start(B("r0i")[:, :], B("IN")["r0"][:, :])), [], [R("r0i")], 2.5, "load r0", sem="lr")
    op("Y", lambda e, B, inc: inc(e.dma_start(B("xs")[:, :], B("IN")["x"][:, :])), [], [R("xs")], 5.0, "load x", sem="lx")
    op("Y", lambda e, B, inc: inc(e.dma_start(B("c0i")[:, :], B("IN")["c0"][:, :])), [], [R("c0i")], 4.0, "load c0", sem="lc")

    def fill(buf, val, n, lo=0):
        v(lambda e, B, inc: inc(e.memset(B(buf)[:, lo:lo + n], val)), [], [R(buf, lo, lo + n)], n / 2)

    def gsel(dst, src, pat, cmp, fillv, base, cm, n, view=None):
        w = slice(0, n) if view is None else view
        gp(lambda e, B, inc: inc(e.affine_select(out=B(dst)[:, w], in_=B(src)[:, w], pattern=pat, compare_op=cmp, fill=fillv, base=base, channel_multiplier=cm)),
           [R(src)], [R(dst)], n, "sel " + dst)

    def scale(dst, src, k):
        n = SCRATCH[src][1][1]
        ts(dst, src, float(k), A.mult, hi=n, cyc=n / 2)

    fill("ones", 1.0, 2048)
    gsel("ey", "ones", [[-1, 128]], A.is_equal, 0.0, 0, 1, 128)
    gsel("b8a", "ones", [[-16, 8]], A.is_ge, 0.0, 0, 1, 8)
    gsel("b8", "b8a", [[16, 8]], A.is_ge, 0.0, 15, -1, 8)
    gsel("b15", "ones", [[-16, 8]], A.is_equal, 0.0, -15, 1, 8)
    scale("ney", "ey", -1)
    fill("mst", 0.0, 144)
    fill("mst15", 0.0, 144)
    for d_, s_ in (("mst", "b8"), ("mst15", "b15")):
        v(lambda e, B, inc, d_=d_, s_=s_: inc(e.tensor_copy(out=B(d_)[:, 15:143:16], in_=B(s_)[:, 0:8])), [R(s_)], [R(d_)], 64)
    scale("mstn", "mst", -1)
    gsel("bo1", "ones", [[-16, 8], [0, 16]], A.is_ge, 0.0, 0, 1, 128)
    gsel("bo", "bo1", [[16, 8], [0, 16]], A.is_ge, 0.0, 15, -1, 128)
    gsel("ux", "bo", [[1, 128]], A.is_gt, 0.0, 0, -1, 128)
    fill("smask", 1.0, CH)
    v(lambda e, B, inc: inc(e.memset(B("smask")[:, 15:CH:16], 0.0)), [], [R("smask")], 64)
    for c in range(NC):
        fill("ka", 0.0, 16, c * KW)
        fill("kb", 0.0, 16, c * KW)
    gsel("u15", "ux", [[0, 8], [-1, 16]], A.is_gt, 0.0, 15, 0, 128)
    scale("u15s", "u15", -SH)
    scale("u15n", "u15", -1)
    gp(lambda e, B, inc: inc(e.iota(B("ki")[:, 0:1], [[0, 1]], 0, 1)), [], [R("ki")], 8)
    gp(lambda e, B, inc: inc(e.iota(B("rio")[:, 0:16], [[1, 16]], 0, 0, allow_small_or_imprecise_dtypes=True)), [], [R("rio")], 16)
    gp(lambda e, B, inc: inc(e.iota(B("dj")[:, 0:32], [[16, 32]], H, 0, allow_small_or_imprecise_dtypes=True)), [], [R("dj")], 32)
    ts("kp", "ki", 15, A.bitwise_and)
    ts("mb", "kp", 16.0, A.mult, -17.0, A.add)
    ts("kd", "ki", 4, A.arith_shift_right)
    tt("ks", "kp", "kd", A.add, 0, 1, 64)
    ts("kw", "ks", 1.0, A.add)
    v(lambda e, B, inc: inc(e.tensor_scalar(out=B("ks")[:, 2:3], in0=B("kw")[:, 0:1], scalar1=15, scalar2=None, op0=A.bitwise_and)), [R("kw")], [R("ks")], 64)
    v(lambda e, B, inc: inc(e.tensor_tensor(out=B("kf")[:, 0:1], in0=B("kp")[:, 0:1], in1=B("ks")[:, 2:3], op=A.min)), [R("kp"), R("ks")], [R("kf", 0, 1)], 64)
    cp("kf", "kp", 1, 2, 64, slo=0)
    ts("dj", "dj", ("kf", 1), A.add, hi=32)
    fill("vm", 0.0, 240)
    ts("vt", "rio", ("kf", 0), A.is_gt, -100.0, A.mult, hi=16)
    ts("ve", "rio", ("kf", 0), A.is_equal, hi=16)
    v(lambda e, B, inc: inc(e.tensor_tensor(out=B("vm")[:, 112:128], in0=B("vt")[:, 0:16], in1=B("ve")[:, 0:16], op=A.add)), [R("vt"), R("ve")], [R("vm")], 64)
    fill("pa", 0.0, 1024)
    gsel("pb", "pa", [[-16, 8], [0, 8], [-1, 16]], A.not_equal, 1.0, 0, 1, 1024)
    gsel("pa", "pb", [[-16, 8], [-1, 8], [-1, 16]], A.not_equal, -1.0, -1, 1, 1024)
    gsel("pb", "pa", [[-16, 8], [-1, 8], [-1, 16]], A.not_equal, -1.0, 15, 1, 1024)
    gsel("pa", "pb", [[-16, 8], [0, 128]], A.is_ge, 0.0, 0, 1, 1024)
    gsel("pb", "pa", [[16, 8], [0, 128]], A.is_ge, 0.0, 15, -1, 1024)
    scale("boq", "bo", 0.25)
    scale("hey", "ey", 0.5)
    tt("boqp", "boq", "hey", A.add, 0, 128, 256)
    tt("boqm", "boq", "hey", A.subtract, 0, 128, 256)
    gsel("tl", "bo", [[-1, 128]], A.is_ge, 0.0, 0, 1, 128)
    scale("tl2", "tl", 2)
    gsel("au", "bo", [[1, 128]], A.is_ge, 0.0, 0, -1, 128)
    scale("au16", "au", 16)
    gsel("hq", "ones", [[-1, 16], [-16, 8], [0, 16]], A.is_equal, 0.0, 0, 1, 2048)
    gsel("mqa", "ones", [[0, 16], [-16, 8]], A.is_ge, 0.0, 0, 1, 128)
    gsel("mq", "mqa", [[1, 16], [16, 8]], A.is_ge, 0.0, -1, -1, 128)
    gsel("mst8", "ones", [[-1, 144]], A.is_equal, 0.0, 15, 16, 144)
    fill("qm", 0.0, 128)
    gsel("qm", "qm", [[-2, 64]], A.not_equal, 0.5, 0, 1, 64, slice(1, 128, 2))
    gsel("qm", "qm", [[-2, 64]], A.not_equal, -0.5, -1, 1, 64, slice(1, 128, 2))
    v(lambda e, B, inc: inc(e.memset(B("qm")[:, 15:128:16], 0.0)), [], [R("qm")], 64)
    tt("qp", "qm", "ey", A.add, 0, 128, 256)
    fill("c1536", float(SH), CH)
    fill("onesf", 1.0, 128)
    fill("zero", 0.0, 8)
    fill("cache", 0.0, P, H)
    cp("cache", "c0i", 0, H, H)
    for i, val in ((2, -40.5), (3, 40.5), (4, -0.5)):
        v(lambda e, B, inc, i=i, val=val: inc(e.memset(B("kf")[:, i:i + 1], val)), [], [R("kf", i, i + 1)], 64)

    def E(B, q, m="mst"):
        return B(m)[:, 15 - q:143 - q]

    def dist(vb, c, pairs, chain, flip):
        ds = tile("B", chain)
        for x in range(CH // W0):
            for i0 in range(0, len(pairs), RT):
                part = pairs[i0:i0 + RT]
                lo, hi = 16 * (c * CH + x * W0), 16 * (c * CH + (x + 1) * W0)
                d = tile("D", chain + "d")
                ad = tile("AD", chain + "a")

                def diff(e, B, inc, part=part, d=d, lo=lo, hi=hi):
                    for i, (p, p2, row) in enumerate(part):
                        o = B(d)[:, i * W0:(i + 1) * W0]
                        inc(e.matmul(o, B("ey")[:, :], B(vb)[:, lo + p:hi:16], True, False))
                        inc(e.matmul(o, B("ney")[:, :], B(vb)[:, lo + p2:hi:16], False, True))
                mm(2 * W0 * len(part), diff, [R(vb, lo, hi), R("ey"), R("ney")], [R(d)], "diff")
                w = W0 * len(part)
                s(lambda e, B, inc, d=d, ad=ad, w=w: inc(e.activation(B(ad)[:, 0:w], B(d)[:, 0:w], F.Abs)), [R(d)], [R(ad)], w, "abs")

                def summ(e, B, inc, part=part, ad=ad, i0=i0, x=x):
                    for i, (p, p2, row) in enumerate(part):
                        inc(e.matmul(B(ds)[:, x * W0:(x + 1) * W0], E(B, row), B(ad)[:, i * W0:(i + 1) * W0], i0 + i == 0, i0 + i == len(pairs) - 1))

                def sumf(e, B, inc, part=part, ad=ad, x=x):
                    b0 = x * W0
                    for i, (p, p2, row) in enumerate(part):
                        inc(e.matmul(B(ds)[:, b0 + row:b0 + 128:16], B(ad)[:, i * W0:i * W0 + 128], B("b8")[:, 0:8], True, True))
                    if part[-1] == pairs[-1]:
                        inc(e.matmul(B(ds)[:, b0 + 15:b0 + 128:16], B(ad)[:, 0:128], B("zero")[:, 0:8], True, True))
                if flip:
                    mm(W0 // 2 * len(part), sumf, [R(ad), R("b8"), R("zero")], [R(ds)], "sum")
                else:
                    mm(W0 * len(part), summ, [R(ad), R("mst")], [R(ds)], "sum")
        return ds

    def gather(vb, off, c):
        for j in range(c * CH, (c + 1) * CH, KG):
            def fn(e, B, inc, j=j):
                o, w = B(vb)[:, 16 * j:16 * (j + KG)], B("xs")[:, 0:W].indirect(B(off)[:, j:j + KG])
                if B("Q") == "V":
                    inc(e.tensor_copy(out=o, in_=w))
                else:
                    inc(e.activation(o, w, F.Copy))
            op(QG.get(cls[0], "VS"), fn, [R("xs"), R(off, j, j + KG)], [R(vb, 16 * j, 16 * (j + KG))], 0.06 + GF * CYC * 16 * KG, "gather")

    def first_fail(ds, c, sbuf, kbuf, ibuf, chain, kacc=None):
        j0, j1, i0 = c * CH, (c + 1) * CH, 16 + c * KW
        s(lambda e, B, inc: inc(e.activation(B(sbuf)[:, j0:j1], B(ds)[:, 0:CH], F.Sign, bias=B("kf")[:, 2:3])), [R(ds), R("kf")], [R(sbuf, j0, j1)], CH, "bad")
        v(lambda e, B, inc: inc(e.tensor_tensor_scan(B(kbuf)[:, i0:i0 + CH], B("smask")[:, 0:CH], B(sbuf)[:, j0:j1], 0.0, A.mult, A.max)),
          [R("smask"), R(sbuf, j0, j1)], [R(kbuf, i0, i0 + CH)], CH / 2, "scan")
        qt = tile("B", chain)

        def fq(e, B, inc):
            for x in range(0, CH, 128):
                inc(e.matmul(B(qt)[:, x:x + 128], B(kbuf)[:, i0 + x:i0 + x + 128], B("ey")[:, :], True, False))
                inc(e.matmul(B(qt)[:, x:x + 128], B(kbuf)[:, i0 + x - 1:i0 + x + 127], B("ney")[:, :], False, True))
        mm(2 * CH, fq, [R("ey"), R("ney"), R(kbuf, i0 - 1, i0 + CH)], [R(qt)], "q")
        if kacc is None:
            def fn(e, B, inc):
                if B("Q") == "S":
                    inc(e.activation(B(ibuf)[:, j0:j1], B(qt)[:, 0:CH], F.Relu))
                else:
                    inc(e.tensor_scalar(out=B(ibuf)[:, j0:j1], in0=B(qt)[:, 0:CH], scalar1=0.0, scalar2=None, op0=A.max))
            op("SV", fn, [R(qt)], [R(ibuf, j0, j1)], 0.06 + CYC * CH, "ind")
        else:
            op("S", lambda e, B, inc: inc(e.activation(B(ibuf)[:, j0:j1], B(qt)[:, 0:CH], F.Relu, accum_out=B("kacc")[:, kacc:kacc + 1])),
               [R(qt)], [R(ibuf, j0, j1), R("kacc", kacc, kacc + 1)], 0.2 + CYC * CH, "ind")

    def phase_a(t, c):
        j0, j1, rf, ch = c * CH, (c + 1) * CH, "rf%d" % t, "A%d_%d" % (t, c)
        if t == 0:
            cp("ru", "r0i", j0, j1, CH)
            ts(rf, "r0i", float(-SH), A.add, lo=j0, hi=j1, cyc=CH)
        else:
            ts("ru", rf, float(SH), A.add, lo=j0, hi=j1, cyc=CH / 2)
        gather("va", "ru", c)
        l15 = tile("B", ch + "r")

        def f15(e, B, inc):
            for q in range(16):
                inc(e.matmul(B(l15)[:, 0:NL], E(B, q, "mst15"), B(rf)[:, j0 + q:j1:16], q == 0, q == 15))
        mm(16 * 64, f15, [R("mst15"), R(rf, j0, j1)], [R(l15)], "r15")
        ts("r15", l15, float(SH), A.add, lo=c * NL, hi=(c + 1) * NL, slo=0, name="r15")
        ds = dist("va", c, [(p, p + 1, p) for p in range(15)], ch, True)
        first_fail(ds, c, "sb", "ka", "ind", ch, t * NC + c if t < RO - 1 else None)

    def phase_b(t, c):
        j0, j1, k0, k1 = c * CH, (c + 1) * CH, c * NL, (c + 1) * NL
        rf, ch = "rf%d" % t, "B%d_%d" % (t, c)
        wm = tile("B", ch)

        def fwm(e, B, inc):
            inc(e.matmul(B(wm)[:, 0:CH], B("ey")[:, :], B(rf)[:, j0:j1], True, False))
            inc(e.matmul(B(wm)[:, 0:CH], B("u15s")[:, :], B("ind")[:, j0:j1], False, True))
            inc(e.matmul(B(wm)[:, CH:2 * CH], B("u15")[:, :], B("ind")[:, j0:j1], True, True))
        mm(3 * CH, fwm, [R("ey"), R("u15"), R("u15s"), R(rf, j0, j1), R("ind", j0, j1)]
           + ([R("kcol", t, t + 1)] if t else []) + ([R("cache")] if t and c else []), [R(wm)], "wm")
        tt("indr", wm, "ind", A.mult, j0, j1, slo=0, name="indr")
        ll = tile("B", ch)

        def ffl(e, B, inc):
            for q in range(16):
                inc(e.matmul(B(ll)[:, NL:2 * NL], E(B, q, "mstn"), B("ind")[:, j0 + q:j1:16], q == 0, False))
            inc(e.matmul(B(ll)[:, NL:2 * NL], B("ey")[:, :], B("ones")[:, 0:NL], False, True))
        mm(17 * 64, ffl, [R("mstn"), R("ey"), R("ones"), R("ind", j0, j1)], [R(ll)], "fail list")

        def frk(e, B, inc):
            for q in range(16):
                inc(e.matmul(B(ll)[:, 0:NL], E(B, q), B("indr")[:, j0 + q:j1:16], q == 0, False))
            inc(e.matmul(B(ll)[:, 0:NL], B("ey")[:, :], B("c1536")[:, 0:NL], False, True))
        mm(17 * 64, frk, [R("mst"), R("ey"), R("c1536"), R("indr", j0, j1)], [R(ll)], "rk list")
        tt("pri", ll, "r15", A.mult, k0, k1, 64, slo=0, name="l")
        if t:
            ts("rkk", ll, ("kcol", t), A.add, lo=k0, hi=k1, slo=0, name="l")
        tt("djn", ll, "dj", A.mult, k0, k1, 64, slo=NL, name="l")
        ts("fi", "pri", 6, A.arith_shift_right, lo=k0, hi=k1, name="l")
        if t:
            tt("si", "rkk", "fi", A.add, k0, k1, 64, name="l")
        else:
            tt("si", ll, "fi", A.add, k0, k1, 64, slo=0, name="l")
        ts("hm", "si", H - 1, A.bitwise_and, lo=k0, hi=k1, name="l")
        tt("hf", "hm", "djn", A.max, k0, k1, 64, name="l")
        cp("hu", "hf", k0, k1, 64, name="hu")
        cls[0] = "P%d%d" % (t, c)
        v(lambda e, B, inc: inc(e.tensor_tensor(out=B("t1")[:, j0:j1], in0=B("cache")[:, 0:H + P].indirect(B("hu")[:, k0:k1]), in1=B(rf)[:, j0:j1], op=A.subtract)),
          [R("cache"), R("hu", k0, k1), R(rf, j0, j1)], [R("t1", j0, j1)], GF * CH, "cache gather")
        tt("t2", wm, "t1", A.mult, j0, j1, slo=CH, name="t2")
        tt("r2", wm, "t2", A.add, j0, j1, slo=0, name="r2")
        gpt, b0 = 1024 // CH, c * 2048
        for g0 in range(0, 8, gpt):
            d = tile("D", ch + "p")

            def fpr(e, B, inc, d=d, g0=g0):
                for i in range(gpt):
                    inc(e.matmul(B(d)[:, i * CH:(i + 1) * CH], B("pb")[:, 128 * (g0 + i):128 * (g0 + i + 1)], B("r2")[:, j0:j1], True, True))
            mm(gpt * CH, fpr, [R("pb"), R("r2", j0, j1)], [R(d)], "pairs")
            ts("eqp", d, 0.0, A.is_equal, lo=b0 + g0 * CH, hi=b0 + (g0 + gpt) * CH, cyc=gpt * CH, slo=0, name="eq")
        vt = tile("B", ch)

        def fv(e, B, inc):
            for g in range(8):
                inc(e.matmul(B(vt)[:, 0:CH], B("vm")[:, 112 - 16 * g:240 - 16 * g], B("eqp")[:, b0 + g * CH:b0 + (g + 1) * CH], g == 0, g == 7))
        mm(8 * CH, fv, [R("vm"), R("eqp", b0, b0 + 8 * CH)], [R(vt)], "V")
        s(lambda e, B, inc: inc(e.activation(B("sf")[:, j0:j1], B(vt)[:, 0:CH], F.Sign, bias=B("kf")[:, 4:5])), [R(vt), R("kf")], [R("sf", j0, j1)], CH, "f")
        rc = tile("B", ch)
        mm(CH, lambda e, B, inc: inc(e.matmul(B(rc)[:, 0:CH], B("ey")[:, :], B("r2")[:, j0:j1], True, True)), [R("ey"), R("r2", j0, j1)], [R(rc)], "copy r2")
        tt("fr", rc, "sf", A.mult, j0, j1, slo=0, name="fr")
        xm = tile("B", ch)

        def fxm(e, B, inc):
            inc(e.matmul(B(xm)[:, 0:CH], B("boqm")[:, :], B("r2")[:, j0:j1], True, False))
            inc(e.matmul(B(xm)[:, 0:CH], B("boq")[:, :], B("fr")[:, j0:j1], False, True))
        mm(2 * CH, fxm, [R("boqm"), R("boq"), R("r2", j0, j1), R("fr", j0, j1)], [R(xm)], "xm")
        ts("ee", xm, 0.0, A.is_equal, lo=j0, hi=j1, cyc=CH, slo=0, name="E")
        v2 = tile("B", ch)

        def fv2(e, B, inc):
            inc(e.matmul(B(v2)[:, 0:CH], B("au16")[:, :], B("sf")[:, j0:j1], True, False))
            inc(e.matmul(B(v2)[:, 0:CH], B("tl2")[:, :], B("ee")[:, j0:j1], False, True))
        mm(2 * CH, fv2, [R("au16"), R("tl2"), R("sf", j0, j1), R("ee", j0, j1)], [R(v2)], "v2")
        s(lambda e, B, inc: inc(e.activation(B("sm")[:, j0:j1], B(v2)[:, 0:CH], F.Sign, bias=B("mb")[:, 0:1])), [R(v2), R("mb")], [R("sm", j0, j1)], CH, "M")
        tt("t3", xm, "sm", A.mult, j0, j1, slo=0, name="t3")
        xp = tile("B", ch)

        def fxp(e, B, inc):
            inc(e.matmul(B(xp)[:, 0:CH], B("boqp")[:, :], B("r2")[:, j0:j1], True, False))
            inc(e.matmul(B(xp)[:, 0:CH], B("boq")[:, :], B("fr")[:, j0:j1], False, True))
        mm(2 * CH, fxp, [R("boqp"), R("boq"), R("r2", j0, j1), R("fr", j0, j1), R("sm", j0, j1)], [R(xp)], "xp")
        tt("rp", xp, "t3", A.add, j0, j1, slo=0, name="rp")
        ts("rpu", "rp", float(SH), A.add, lo=j0, hi=j1, cyc=CH / 2, name="rpu")

    def hrep(t, c):
        j0, j1, k0, k1 = c * CH, (c + 1) * CH, c * NL, (c + 1) * NL
        cp("hh", "hf", k0, k1, 64, name="hh")
        hr = tile("B", "H%d_%d" % (t, c))

        def fh(e, B, inc):
            for q in range(16):
                inc(e.matmul(B(hr)[:, q:CH:16], B("hq")[:, 128 * q:128 * (q + 1)], B("hh")[:, k0:k1], True, True))
        mm(16 * 64, fh, [R("hq"), R("hh", k0, k1)], [R(hr)], "hrep")
        cp("hrep", hr, j0, j1, CH, slo=0, name="hrep")

    def winners(t):
        if t < RO - 1:
            kt = tile("B", "K%d" % t)

            def fk(e, B, inc):
                for c in range(NC):
                    inc(e.matmul(B(kt)[:, 0:1], B("onesf")[:, :], B("kacc")[:, t * NC + c:t * NC + c + 1], c == 0, c == NC - 1))
            mm(256 * NC, fk, [R("onesf"), R("kacc", t * NC, t * NC + NC)], [R(kt)], "K")
            cp("kcol", kt, t + 1, t + 2, 64, slo=0, name="K")
        for k in range(32):
            n = P - 16 * k
            v(lambda e, B, inc, k=k, n=n: inc(e.tensor_scalar(out=B("eqw")[:, P * k:P * k + n], in0=B("hrep")[:, 16 * k:P], scalar1=B("hf")[:, k:k + 1], scalar2=None, op0=A.is_equal)),
              [R("hrep", 16 * k, P), R("hf", k, k + 1)], [R("eqw", P * k, P * k + n)], n / 2, "win")
        z = tile("B", "W%d" % t)
        for k0 in range(0, 32, 4):
            def fz(e, B, inc, k0=k0):
                if k0 == 0:
                    inc(e.matmul(B(z)[0:8, 0:P], B("zero")[:, 0:8], B("eqw")[:, 0:P], True, False))
                for k in range(k0, min(k0 + 4, 31)):
                    inc(e.matmul(B(z)[0:8, 16 * (k + 1):P], B("b8")[:, 0:8], B("eqw")[:, P * k + 16:P * k + P - 16 * k], False, False))
            mm(4 * (P - 16 * k0), fz, [R("zero"), R("b8"), R("eqw", P * k0, P * (k0 + 3) + P - 16 * (k0 + 3))], [R(z)], "Z")

        def fzd(e, B, inc):
            for q in range(16):
                inc(e.matmul(B(z)[0:8, q:P:16], B("mq")[:, 8 * q:8 * q + 8], B("eqw")[:, q:32 * P:P], False, q == 15))
        mm(16 * 32, fzd, [R("mq"), R("eqw")], [R(z)], "Zd")
        s(lambda e, B, inc: inc(e.activation(B("lose")[0:8, 0:P], B(z)[0:8, 0:P], F.Sign)), [R(z)], [R("lose")], P, "lose")
        wl = tile("B", "W%d" % t)

        def fl(e, B, inc):
            for q in range(16):
                inc(e.matmul(B(wl)[:, 0:32], B("mst8")[0:8, 15 - q:143 - q], B("lose")[0:8, q:P:16], q == 0, q == 15))
        mm(16 * 64, fl, [R("mst8"), R("lose")], [R(wl)], "lose list")
        tt("lt", wl, "dj", A.mult, 0, 32, 64, name="w")
        tt("lo", "lt", "hf", A.max, 0, 32, 64, name="w")
        cp("wu", "lo", 0, 32, 64, name="w")

    def phase_d(t, c):
        ch = "D%d_%d" % (t, c)
        gather("vd", "rpu", c)
        ds = dist("vd", c, [(p, p + 1, p) for p in range(15)], ch, True)
        first_fail(ds, c, "sb2", "kb", "ind2", ch)
        cls[0] = "N%d%d" % (t, c)
        return dist("vd", c, [(p, p + 2, p + 1) for p in range(0, 14, 2)], ch + "n", False)

    def phase_e(t, c, dn):
        j0, j1, ch = c * CH, (c + 1) * CH, "E%d_%d" % (t, c)
        s(lambda e, B, inc: inc(e.activation(B("sn")[:, j0:j1], B(dn)[:, 0:CH], F.Sign, scale=-1.0, bias=B("kf")[:, 3:4])), [R(dn), R("kf")], [R("sn", j0, j1)], CH, "near")
        n1 = tile("B", ch + "n")

        def f6(e, B, inc):
            inc(e.matmul(B(n1)[:, 0:CH], B("qm")[:, :], B("rp")[:, j0:j1], True, True))
            inc(e.matmul(B(n1)[:, CH:2 * CH], B("qp")[:, :], B("rp")[:, j0:j1], True, t < RO - 1))
            if t == RO - 1:
                inc(e.matmul(B(n1)[:, CH:2 * CH], B("ey")[:, :], B("c1536")[:, :], False, True))
        mm(2 * CH, f6, [R("qm"), R("qp"), R("ey"), R("c1536"), R("rp", j0, j1), R("sn", j0, j1)], [R(n1)], "n1")
        tt("t5", n1, "sn", A.mult, j0, j1, slo=0, name="t5")
        out = "yrs" if t == RO - 1 else "rn%d" % t
        tt(out, n1, "t5", A.add, j0, j1, slo=CH, name="rn")
        if t == RO - 1:
            op("Y", lambda e, B, inc: inc(e.dma_start(B("IN")["yr"][:, j0:j1], B("yrs")[:, j0:j1])), [R("yrs", j0, j1)], [("yr", j0, j1)], 2.5, "store yr", sem="oy%d" % c)
        else:
            op("G", ("send", t, c, j0, j1), [R(out, j0, j1)], [], 1.0, "send", sem="ls%d_%d" % (t + 1, c))
            ops[-1]["sem2"] = "ar%d_%d" % (t + 1, c)
            op("N", ("arrive", t + 1, c), [R(out, j0, j1)], [R("rf%d" % (t + 1), j0, j1)], 3.5, "arrive", sem="ar%d_%d" % (t + 1, c))
            ops[-1]["after"] = len(ops) - 2
        cls[0] = "S%d%d" % (t, c)
        om = tile("B", ch)

        def fom(e, B, inc):
            inc(e.matmul(B(om)[:, 0:CH], B("ey")[:, :], B("ones")[:, 0:CH], True, False))
            inc(e.matmul(B(om)[:, 0:CH], B("u15n")[:, :], B("ind2")[:, j0:j1], False, True))
            inc(e.matmul(B(om)[:, CH:2 * CH], B("ey")[:, :], B("rp")[:, j0:j1], True, True))
        mm(3 * CH, fom, [R("ey"), R("ones"), R("u15n"), R("ind2", j0, j1), R("rp", j0, j1)], [R(om)], "om")
        tt("indr2", om, "ind2", A.mult, j0, j1, slo=CH, name="indr2")
        tt("t4", om, "rp", A.mult, j0, j1, slo=0, name="t4")
        sk = tile("B", ch)

        def fsk(e, B, inc):
            inc(e.matmul(B(sk)[:, 0:CH], B("ey")[:, :], B("c1536")[:, :], True, False))
            inc(e.matmul(B(sk)[:, 0:CH], B("u15")[:, :], B("indr2")[:, j0:j1], False, True))
        mm(2 * CH, fsk, [R("ey"), R("c1536"), R("u15"), R("indr2", j0, j1)], [R(sk)], "sk")
        tt("st", sk, "t4", A.add, j0, j1, slo=0, name="st")
        k0, k1 = c * NL, (c + 1) * NL
        v(lambda e, B, inc: inc(e.tensor_copy(out=B("cache")[:, 0:H + P].indirect(B("wu")[:, k0:k1]), in_=B("st")[:, j0:j1])),
          [R("wu", k0, k1), R("st", j0, j1)], [R("cache")], SCF * CH, "scatter")

    for t in range(RO):
        for c in range(NC):
            cls[0] = "A%d%d" % (t, c)
            phase_a(t, c)
        for c in range(NC):
            cls[0] = "B%d%d" % (t, c)
            phase_b(t, c)
            cls[0] = "H%d%d" % (t, c)
            hrep(t, c)
        cls[0] = "W%d0" % t
        winners(t)
        for c in range(NC):
            cls[0] = "D%d%d" % (t, c)
            dn = phase_d(t, c)
            cls[0] = "E%d%d" % (t, c)
            phase_e(t, c, dn)
    op("Y", lambda e, B, inc: inc(e.dma_start(B("IN")["yc"][:, :], B("cache")[:, 0:H])), [R("cache", 0, H)], [("yc", 0, H)], 3.0, "store yc", sem="oc")
    return ops, tiles


def deps_of(ops, key, cross):
    hist, out = {}, []
    for o in ops:
        d = {}
        for rw, regs in (("r", o["r"]), ("w", o["w"])):
            for (b, lo, hi) in regs:
                for (lo2, hi2, rw2, o2) in hist.get(key(b), ()):
                    if o2 is o or lo2 >= hi or hi2 <= lo:
                        continue
                    kind = rw2 + rw
                    if kind == "rr" and not (cross(b) and o2["q"] != o["q"]):
                        continue
                    d.setdefault(o2["id"], set()).add((kind, cross(b)))
        if "after" in o:
            d.setdefault(o["after"], set()).add(("wr", False))
        for rw, regs in (("r", o["r"]), ("w", o["w"])):
            for (b, lo, hi) in regs:
                h = hist.setdefault(key(b), [])
                if rw == "w" and not cross(b):
                    h[:] = [x for x in h if not (lo <= x[0] and x[1] <= hi)]
                h.append((lo, hi, rw, o))
        out.append(d)
    return out


PSUM = set(k for k in SCRATCH if SCRATCH[k][0] == "psum")


def is_tile(b):
    return b in PSUM


def schedule():
    ops, tiles = build_ops()
    for o in ops:
        o["q"] = o["qs"][0]
        for b, lo, hi in o["r"] + o["w"]:
            if isinstance(b, tuple):
                tiles[b[1]]["users"] += 1
    dep = deps_of(ops, lambda b: b, lambda b: isinstance(b, tuple) and tiles[b[1]]["pool"] != "AD")
    n = len(ops)
    succ = [[] for _ in range(n)]
    left = [len(dep[i]) for i in range(n)]
    for i in range(n):
        for d in dep[i]:
            succ[d].append(i)
    rank = [0.0] * n
    for i in range(n - 1, -1, -1):
        rank[i] = ops[i]["dur"] + max([rank[j] + LAT for j in succ[i]] or [0.0])
    for i in range(n):
        rank[i] += BIAS.get(ops[i]["cls"], 0.0)
    free = {q: 0.0 for q in "VSTGYAN"}
    pool = {k: {b: 0.0 for b in v_} for k, v_ in POOLS.items()}
    live, endt, order = {}, [0.0] * n, []
    ready = [i for i in range(n) if left[i] == 0]
    while ready:
        cands = []
        for i in ready:
            o = ops[i]
            est0 = max([endt[d] + (LAT if any(k != "rw" for k, _ in kk) or ops[d]["q"] != o["qs"][0] else 0.0) for d, kk in dep[i].items()] or [0.0])
            okay = True
            for b, lo, hi in o["w"]:
                if isinstance(b, tuple) and tiles[b[1]]["buf"] is None:
                    tl = tiles[b[1]]
                    fr = pool[tl["pool"]]
                    if not fr or (tl["pool"] == "B" and len(fr) < 2 and not live.get(tl["chain"], 0)):
                        okay = False
                    else:
                        est0 = max(est0, min(fr.values()) + LAT)
            if okay:
                for q in o["qs"]:
                    cands.append((max(est0, free[q] if q != "N" else 0.0), -rank[i], i, q))
        assert cands, "no operation can go on"
        t0 = min(c[0] for c in cands)
        st, _, i, q = min([c for c in cands if c[0] <= t0 + 0.03], key=lambda c: (c[1], c[0]))
        o = ops[i]
        o["q"] = q
        for b, lo, hi in o["w"]:
            if isinstance(b, tuple) and tiles[b[1]]["buf"] is None:
                tl = tiles[b[1]]
                fr = pool[tl["pool"]]
                bb = min(fr, key=lambda x: fr[x])
                del fr[bb]
                tl["buf"] = bb
                live[tl["chain"]] = live.get(tl["chain"], 0) + 1
        e = st + o["dur"]
        endt[i], o["t0"], o["t1"] = e, st, e
        free[q] = st + 0.1 if q in "YA" else e
        if q == "A":
            free["S"] = max(free["S"], 0.1)
        for b, lo, hi in o["r"] + o["w"]:
            if isinstance(b, tuple):
                tl = tiles[b[1]]
                tl["users"] -= 1
                tl["end"] = max(tl.get("end", 0.0), e)
                if tl["users"] == 0:
                    pool[tl["pool"]][tl["buf"]] = tl["end"]
                    live[tl["chain"]] -= 1
        order.append(i)
        ready.remove(i)
        for j in succ[i]:
            left[j] -= 1
            if left[j] == 0:
                ready.append(j)
    assert len(order) == n
    return [ops[i] for i in order], tiles, max(endt)


PLAN = {}


def plan():
    if not PLAN:
        seq, tiles, end = schedule()
        key = lambda b: tiles[b[1]]["buf"] if isinstance(b, tuple) else b
        PLAN["seq"], PLAN["tiles"], PLAN["end"] = seq, tiles, end
        PLAN["dep"] = deps_of(seq, key, lambda b: is_tile(key(b)))
    return PLAN


def rank_program(g, core, T, topo):
    rank = T.rank_of(core)
    if rank is None:
        return
    pl = plan()
    tiles = pl["tiles"]
    dst = T.cores[(rank + ST) % len(T.cores)]
    src = T.cores[(rank - ST) % len(T.cores)]
    rid, pid, _ = topo.addr(dst)
    emask, ne, ne_in = topo.mask(core, dst), len(topo.engines(core, dst)), len(topo.engines(src, core))
    eng = {"V": g.vector, "S": g.scalar, "T": g.tensor, "G": g, "Y": g.sync, "A": g.scalar}
    host = {"V": "V", "S": "S", "T": "T", "G": "G", "Y": "Y", "A": "S"}
    ins = {"x": T.x, "r0": T.r0, "c0": T.c0, "yc": T.yc, "yr": T.yr}
    cur = ["V"]

    def B(name):
        if name == "Q":
            return cur[0]
        if name == "IN":
            return ins
        return T[tiles[name[1]]["buf"]] if isinstance(name, tuple) else T[name]

    cnt = {"V": 0, "S": 0, "T": 0, "G": 0}
    known = {q: {} for q in "VSTGY"}
    done, pend = {}, {}

    def inc(x, q):
        cnt[q] += 1
        x.then_inc(T.sem["q" + q], 1)

    for o, dep in zip(pl["seq"], pl["dep"]):
        q = o["q"]
        if q == "N":
            done[o["id"]] = (o["sem"], ne_in, {})
            pend[o["sem"]] = ne_in
            continue
        h = host[q]
        kn, need = known[h], {}
        for d, kinds in dep.items():
            sem, c, imp = done[d]
            if sem == "q" + h:
                if (h == "T" and all(cr for _, cr in kinds)) or all(k == "rw" for k, _ in kinds):
                    continue
            if c > need.get(sem, (0, None))[0]:
                need[sem] = (c, imp)
        for sem in sorted(need, key=lambda x: -need[x][0]):
            c, imp = need[sem]
            if kn.get(sem, 0) >= c:
                continue
            eng[q].wait_ge(T.sem[sem], c)
            kn[sem] = c
            for s2, c2 in imp.items():
                kn[s2] = max(kn.get(s2, 0), c2)
        cur[0] = q
        if isinstance(o["fn"], tuple):
            _, t, c, j0, j1 = o["fn"]
            g.remote_dma(T["rf%d" % (t + 1)][:, j0:j1], T["rn%d" % t][:, j0:j1], T.sem[o["sem2"]], T.sem[o["sem"]], pid, rid, emask)
            done[o["id"]] = (o["sem"], ne, {})
            pend[o["sem"]] = ne
        elif o["sem"]:
            o["fn"](eng[q], B, lambda x: x.then_inc(T.sem[o["sem"]], 16))
            done[o["id"]] = (o["sem"], 16, dict(kn))
            pend[o["sem"]] = 16
        else:
            o["fn"](eng[q], B, lambda x: inc(x, h))
            imp = dict(kn)
            imp["q" + h] = cnt[h]
            done[o["id"]] = ("q" + h, cnt[h], imp)
    for q in "VSTG":
        g.wait_ge(T.sem["q" + q], cnt[q])
    for sname in pend:
        if known["G"].get(sname, 0) < pend[sname]:
            g.wait_ge(T.sem[sname], pend[sname])
